import numpy as np
import ml_dtypes


def mxq(x, axis, fmt="e4m3"):
    dtype, down = {"e4m3": (ml_dtypes.float8_e4m3fn, 7), "e5m2": (ml_dtypes.float8_e5m2, 14)}[fmt]
    v = np.moveaxis(np.asarray(x, np.float32).astype(ml_dtypes.bfloat16).astype(np.float64), axis, -1)
    blocks = v.reshape(v.shape[:-1] + (-1, 32))
    amax = np.abs(blocks).max(-1, keepdims=True)
    byte = np.maximum(np.where(amax > 0, np.frexp(amax)[1] - 1 + 127, 0) - down, 1)
    scale = np.exp2(byte - 127.0)
    codes = (blocks / scale).astype(np.float32).astype(dtype).astype(np.float64)
    return np.moveaxis((codes * scale).reshape(v.shape), -1, axis)


WIDE = False


def mx_kscale(k):
    if not WIDE:
        return np.ones(k)
    levels = np.array([10, -10, 5, -5, 0])
    if k % 512:
        return np.exp2(np.random.permutation(np.resize(levels, k // 32))).repeat(32)
    a = np.empty((k // 512, 16))
    for p in range(k // 512):
        a[p, :8] = np.random.permutation(np.resize(levels, 8))
        for g in range(8):
            far = levels[np.abs(levels - a[p, g]) >= 10]
            a[p, g + 8] = far[np.random.randint(len(far))]
    return np.exp2(a.ravel()).repeat(32)


def f64(x):
    return np.asarray(x).astype(np.float64)


def striped(idx):
    return np.tile(idx.reshape(-1, 16).T, (8, 1)).astype(np.uint16)


def unstriped(offs):
    return offs[:16].T.reshape(-1).astype(np.int64)


def gelu(v):
    return 0.5 * v * (1.0 + np.tanh(np.sqrt(2.0 / np.pi) * (v + 0.044715 * v**3)))


K, T, E, C, H, N = 512, 640, 4, 256, 512, 128
PAD = 32


def by_expert(wq, xq):
    return np.concatenate([wq[e].T @ xq[:, e * C:(e + 1) * C] for e in range(E)], axis=1)


def setup_inputs():
    n = np.random.standard_normal
    s = mx_kscale(K)[:, None]
    u = mx_kscale(H)
    first = np.random.permutation(np.repeat(np.arange(E), T // E))
    second = (first + 1 + np.random.permutation(np.repeat(np.arange(E - 1), -(-T // (E - 1)))[:T])) % E
    while np.bincount(second, minlength=E).max() != T // E:
        load = np.bincount(second, minlength=E); hi, lo = int(load.argmax()), int(load.argmin())
        t = np.flatnonzero((second == hi) & (first != lo))[0]; second[t] = lo
    slot_token = np.empty(E * C, np.int64); pos = np.empty((2, T), np.int64); fill = np.zeros(E, np.int64)
    place = np.stack([np.random.permutation(C) for _ in range(E)])
    for r, deal in enumerate((first, second)):
        for t in np.random.permutation(T):
            e = deal[t]
            if fill[e] < C: j = e * C + place[e, fill[e]]; fill[e] += 1; slot_token[j] = t; pos[r, t] = j
            else: pos[r, t] = E * C + t % PAD
    g = np.random.uniform(0.2, 0.8, T)
    return {
        "xT": (n((K, T)) * s).astype(np.float32),
        "w1": (n((E, K, H)) / np.sqrt(K) / s[None]).astype(np.float32),
        "w3": (n((E, K, H)) / np.sqrt(K) / s[None] * u[None, None, :]).astype(np.float32),
        "w2": (n((E, H, N)) / np.sqrt(H) / u[None, :, None]).astype(np.float32),
        "gate": np.stack([np.tile(g, (N, 1)), np.tile(1.0 - g, (N, 1))]).astype(np.float32),
        "offs": striped(slot_token),
        "pos1": striped(pos[0]),
        "pos2": striped(pos[1]),
    }


def reference(xT, w1, w3, w2, gate, offs, pos1, pos2):
    idx = unstriped(offs)
    xq = mxq(f64(xT)[:, idx], 0, "e4m3")
    h = gelu(by_expert(mxq(f64(w1), 1, "e4m3"), xq))
    h = h * by_expert(mxq(f64(w3), 1, "e4m3"), xq)
    y = by_expert(mxq(f64(w2), 1, "e4m3"), mxq(h, 0, "e4m3"))
    y = np.concatenate([y, np.zeros((N, PAD))], axis=1)
    return f64(gate[0]) * y[:, unstriped(pos1)] + f64(gate[1]) * y[:, unstriped(pos2)]

@@ -1,0 +1,251 @@
+from contextlib import ExitStack
+
+import concourse.mybir as mybir
+
+F32 = mybir.dt.float32
+BF16 = mybir.dt.bfloat16
+I32 = mybir.dt.int32
+U32 = mybir.dt.uint32
+U16 = mybir.dt.uint16
+U8 = mybir.dt.uint8
+FP8X4 = mybir.dt.float8_e4m3fn_x4
+MULT = mybir.AluOpType.mult
+ADD = mybir.AluOpType.add
+GELU = mybir.ActivationFunctionType.Gelu_apprx_tanh
+
+P = 128
+K, T, E, C, H, N = 512, 640, 4, 256, 512, 128
+S = E * C
+PAD = 32
+WIN = 704
+FLOPS = 2 * S * K * H * 2 + 2 * S * H * N
+MS1 = (128, 80, 80, 56)
+MS3 = ((80,), (80,), (80,), (40, 24))
+CUTS3 = (((0, P),), ((0, P),), ((0, P),), ((0, 64), (64, P)))
+W2S = (1, 2)
+W2_LOAD = (3, 3)
+W2_AT = (3, 3)
+Y_GROUPS = ((0, 1), (2,), (3,))
+Y_AT = {(0, 1): 3, (2,): 3, (3,): 3}
+XCH = ((256, 0), (256, 128), (128, 0))
+
+
+def tile_moe_cap2_glu_gelu_kernel(tc, xT, w1, w3, w2, gate, offs, pos1, pos2, out):
+    nc = tc.nc
+    with ExitStack() as ctx:
+        lists = ctx.enter_context(tc.tile_pool(name="lists", bufs=1))
+        keep = ctx.enter_context(tc.tile_pool(name="keep", bufs=1))
+        work = ctx.enter_context(tc.tile_pool(name="work", bufs=4))
+        psum = ctx.enter_context(tc.psum_pool(name="psum", bufs=3))
+        psum_y = ctx.enter_context(tc.psum_pool(name="psum_y", bufs=2))
+
+        offs_t = lists.tile([P, S // 16], U16, name="offs_t")
+        pos1_t = lists.tile([P, T // 16], U16, name="pos1_t")
+        pos2_t = lists.tile([P, T // 16], U16, name="pos2_t")
+
+        xv = xT.rearrange("(p j) t -> p j t", j=4)
+        xr = []
+        lo = 0
+        for width, s_cols in XCH:
+            xc = keep.tile([P, 4, width], F32, name=f"x{lo}")
+            nc.sync.dma_start(xc[:], xv[:, :, lo : lo + width])
+            xr.append(xc)
+            lo += width
+        nc.sync.dma_start(offs_t[:], offs)
+        r1, r3, r2 = [], [], []
+        gates = [keep.tile([P, T], F32, name=f"gate{c}") for c in range(2)]
+        w2v = w2.rearrange("e (p j) n -> p e j n", j=4)
+
+        def load_w2(pair):
+            c = keep.tile([P, 2, 4, N], F32, name=f"r2_{pair}")
+            nc.sync.dma_start(c[:], w2v[:, 2 * pair : 2 * pair + 2])
+            r2.append(c)
+
+        for e in range(E):
+            a = keep.tile([P, 4, H], F32, name=f"r1_{e}")
+            nc.sync.dma_start(a[:], w1[e].rearrange("(p j) i -> p j i", j=4))
+            w3e = w3[e].rearrange("(p j) i -> p j i", j=4)
+            parts = []
+            for lo, hi in CUTS3[e]:
+                b = keep.tile([P, 4, 4 * (hi - lo)], F32, name=f"r3_{e}_{lo}")
+                nc.sync.dma_start(b[:], w3e[:, :, 4 * lo : 4 * hi])
+                parts.append(b)
+            r1.append([a])
+            r3.append(parts)
+            for pair in range(2):
+                if W2_LOAD[pair] == e:
+                    load_w2(pair)
+        nc.sync.dma_start(pos1_t[:], pos1)
+        nc.sync.dma_start(pos2_t[:], pos2)
+        for c in range(2):
+            nc.sync.dma_start(gates[c][:], gate[c])
+
+        xs = keep.tile([P, WIN], U8, name="xs", align_bytes=64)
+        nc.gpsimd.memset(xs[:], 0)
+        xq = keep.tile([P, WIN], I32, name="xq", align_bytes=64)
+        nc.vector.memset(xq[:, T:WIN], 0)
+        ys = keep.tile([P, S + PAD], F32, name="ys")
+        nc.vector.memset(ys[:, S : S + PAD], 0.0)
+        dummy = keep.tile([P, 1], F32, name="dummy")
+        nc.vector.memset(dummy[:], 0.0)
+        dummy2 = keep.tile([P, 1], F32, name="dummy2")
+        nc.scalar.activation(out=dummy2[:], in_=dummy[:], func=GELU)
+
+        xb = keep.tile([P, T, 4], BF16, name="xb", align_bytes=64)
+
+        def turn(engine_copy, dst, src):
+            engine_copy(
+                out=dst.rearrange("p (c i) j -> p c j i", i=4),
+                in_=src.rearrange("p j (c i) -> p c j i", i=4),
+            )
+
+        lo = 0
+        for (width, s_cols), xc in zip(XCH, xr):
+            if s_cols:
+                turn(nc.scalar.copy, xb[:, lo : lo + s_cols, :], xc[:, :, 0:s_cols])
+            if s_cols < width:
+                turn(nc.vector.tensor_copy, xb[:, lo + s_cols : lo + width, :], xc[:, :, s_cols:width])
+            nc.vector.quantize_mx(
+                out=xq[:, lo : lo + width].bitcast(FP8X4),
+                scales=xs[:, lo : lo + width],
+                in_=xb[:, lo : lo + width, :].rearrange("p t j -> p (t j)"),
+            )
+            lo += width
+
+        def prepare(raws, tag, cuts, shares):
+            wb = work.tile([P, 4, P, 4], BF16, name=tag + "b", align_bytes=64)
+            wq = work.tile([P, 4, P], U32, name=tag + "q", align_bytes=64)
+            ws = work.tile([P, 4, P], U8, name=tag + "s", align_bytes=64)
+            for raw, (lo, hi), share in zip(raws, cuts, shares):
+                for copy, c0, c1 in ((nc.scalar.copy, lo, lo + share), (nc.vector.tensor_copy, lo + share, hi)):
+                    if c0 < c1:
+                        copy(
+                            out=wb[:, :, c0:c1, :].rearrange("p (u v) m j -> p u m j v", v=2),
+                            in_=raw[:, :, 4 * (c0 - lo) : 4 * (c1 - lo)].rearrange("p j (m u v) -> p u m j v", u=2, v=2),
+                        )
+                if hi - lo == P:
+                    nc.vector.quantize_mx(
+                        out=wq[:].rearrange("p t m -> p (t m)").bitcast(FP8X4),
+                        scales=ws[:].rearrange("p t m -> p (t m)"),
+                        in_=wb[:].rearrange("p t m j -> p (t m j)"),
+                    )
+                else:
+                    for t in range(4):
+                        nc.vector.quantize_mx(
+                            out=wq[:, t, lo:hi].bitcast(FP8X4),
+                            scales=ws[:, t, lo:hi],
+                            in_=wb[:, t, lo:hi, :].rearrange("p m j -> p (m j)"),
+                        )
+            return wq, ws
+
+        def gather(e, count):
+            xgw = work.tile([P, count * C], U32, name="xgw", align_bytes=64)
+            xgs = work.tile([P, count * C], U8, name="xgs", align_bytes=64)
+            cols = slice(e * C // 16, (e + count) * C // 16)
+            nc.vector.tensor_copy(xgw[:], xq[:].bitcast(U32).indirect(offs_t[:, cols]))
+            nc.vector.tensor_copy(xgs[:], xs[:].indirect(offs_t[:, cols]))
+            return [(xgw[:, i * C : (i + 1) * C], xgs[:, i * C : (i + 1) * C]) for i in range(count)]
+
+        def project(weights, tokens, tag):
+            wq, ws = weights
+            xgw, xgs = tokens
+            banks = []
+            for half in range(2):
+                acc = psum.tile([P, 4, P], F32, name=tag)
+                sl = slice(half * P, (half + 1) * P)
+                for t in range(4):
+                    nc.tensor.matmul_mx(
+                        out=acc[:, t, :],
+                        lhsT=wq[:, t, :].bitcast(FP8X4),
+                        lhsT_scale=ws[:, t, :],
+                        rhs=xgw[:, sl].bitcast(FP8X4),
+                        rhs_scale=xgs[:, sl],
+                        start=True,
+                        stop=True,
+                    )
+                banks.append(acc)
+            return banks
+
+        def prepare_w2(pair):
+            w2b = work.tile([P, 2, N, 4], BF16, name="w2b", align_bytes=64)
+            w2q = work.tile([P, 2 * N], U32, name="w2q", align_bytes=64)
+            w2s = work.tile([P, 2 * N], U8, name="w2s", align_bytes=64)
+            for i in range(2):
+                turn(nc.scalar.copy if i < W2S[pair] else nc.vector.tensor_copy, w2b[:, i], r2[pair][:, i])
+            nc.vector.quantize_mx(
+                out=w2q[:].bitcast(FP8X4), scales=w2s[:], in_=w2b[:].rearrange("p e n j -> p (e n j)")
+            )
+            return [(w2q[:, i * N : (i + 1) * N], w2s[:, i * N : (i + 1) * N]) for i in range(2)]
+
+        def finish(acc, weights, hidden, pieces):
+            w2q, w2s = weights
+            hq, hs = hidden
+            for sl in pieces:
+                nc.tensor.matmul_mx(
+                    out=acc[:, sl],
+                    lhsT=w2q.bitcast(FP8X4),
+                    lhsT_scale=w2s,
+                    rhs=hq[:, sl].bitcast(FP8X4),
+                    rhs_scale=hs[:, sl],
+                    start=True,
+                    stop=True,
+                )
+
+        halves = (slice(0, P), slice(P, C))
+        whole = (slice(0, C),)
+        hidden = []
+        w2qs = {}
+        tokens = {}
+        tokens[0], tokens[1] = gather(0, 2)
+        for e in range(E):
+            if e == 1:
+                tokens[2], tokens[3] = gather(2, 2)
+            banks_a = project(prepare(r1[e], "w1", ((0, P),), (MS1[e],)), tokens[e], "acc_a")
+            w3qs = prepare(r3[e], "w3", CUTS3[e], MS3[e])
+            gs = []
+            for half in range(2):
+                g = work.tile([P, P, 4], F32, name="g")
+                nc.scalar.activation(out=g[:], in_=banks_a[half][:].rearrange("p t n -> p n t"), func=GELU)
+                gs.append(g)
+            banks_b = project(w3qs, tokens[e], "acc_b")
+            for pair in range(2):
+                if W2_AT[pair] == e:
+                    w2qs[2 * pair], w2qs[2 * pair + 1] = prepare_w2(pair)
+            hb = work.tile([P, C, 4], BF16, name="hb", align_bytes=64)
+            hq = work.tile([P, C], U32, name="hq", align_bytes=64)
+            hs = work.tile([P, C], U8, name="hs", align_bytes=64)
+            for half in range(2):
+                nc.vector.tensor_tensor(
+                    out=hb[:, halves[half], :], in0=gs[half][:], in1=banks_b[half][:].rearrange("p t n -> p n t"), op=MULT
+                )
+            pieces = halves if e == E - 1 else whole
+            for sl in pieces:
+                nc.vector.quantize_mx(
+                    out=hq[:, sl].bitcast(FP8X4), scales=hs[:, sl], in_=hb[:, sl, :].rearrange("p n j -> p (n j)")
+                )
+            hidden.append((hq, hs))
+            for group in Y_GROUPS:
+                if e == Y_AT[group]:
+                    y = psum_y.tile([P, 2 * C], F32, name="y")
+                    for i, f in enumerate(group):
+                        finish(y[:, i * C : (i + 1) * C], w2qs[f], hidden[f], halves if f == E - 1 else whole)
+                    lo = group[0] * C
+                    hi = lo + len(group) * C
+                    cut = lo + P if e == E - 1 and group == (E - 1,) else hi
+                    nc.scalar.copy(out=ys[:, lo:cut], in_=y[:, 0 : cut - lo])
+                    if cut < hi:
+                        nc.scalar.copy(out=ys[:, cut:hi], in_=y[:, cut - lo : hi - lo])
+
+        cuts = (0, 448, T)
+        toks = [slice(cuts[i], cuts[i + 1]) for i in range(2)]
+        z1 = keep.tile([P, T], F32, name="z1")
+        nc.vector.tensor_tensor(z1[:], ys[:].indirect(pos1_t[:]), gates[0][:], MULT)
+        z2 = []
+        for i in range(2):
+            z2.append(keep.tile([P, cuts[i + 1] - cuts[i]], F32, name=f"z2_{i}"))
+            cols = slice(cuts[i] // 16, cuts[i + 1] // 16)
+            nc.vector.tensor_tensor(z2[i][:], ys[:].indirect(pos2_t[:, cols]), gates[1][:, toks[i]], MULT)
+        for i in range(2):
+            total = keep.tile([P, cuts[i + 1] - cuts[i]], F32, name=f"total{i}")
+            nc.vector.tensor_tensor(total[:], z1[:, toks[i]], z2[i][:], ADD)
+            nc.sync.dma_start(out[:, toks[i]], total[:])

@@ -19,15 +19,18 @@ S = E * C
 PAD = 32
 WIN = 704
 FLOPS = 2 * S * K * H * 2 + 2 * S * H * N
-MS1 = (128, 80, 80, 56)
-MS3 = ((80,), (80,), (80,), (40, 24))
-CUTS3 = (((0, P),), ((0, P),), ((0, P),), ((0, 64), (64, P)))
-W2S = (1, 2)
-W2_LOAD = (3, 3)
-W2_AT = (3, 3)
-Y_GROUPS = ((0, 1), (2,), (3,))
-Y_AT = {(0, 1): 3, (2,): 3, (3,): 3}
-XCH = ((256, 0), (256, 128), (128, 0))
+S1 = (128, 40, 40, 64)
+S3 = (128, 88, 88, 64)
+GROUPS = ((0, 1), (2, 3))
+GBUFS = 2
+W2_GROUPS = ((0,), (1,), (2,), (3,))
+W2_LOAD = (4, 4, 4, 4)
+W2_S = (1, 0, 1, 1)
+LAG = (0, 0, 0)
+YV = 0
+Y_GROUPS = ((0, 1), (2,))
+CUT = 384
+XCH = ((384, 128), (256, 96))
 
 
 def tile_moe_cap2_glu_gelu_kernel(tc, xT, w1, w3, w2, gate, offs, pos1, pos2, out):
@@ -36,6 +39,7 @@ def tile_moe_cap2_glu_gelu_kernel(tc, xT, w1, w3, w2, gate, offs, pos1, pos2, ou
         lists = ctx.enter_context(tc.tile_pool(name="lists", bufs=1))
         keep = ctx.enter_context(tc.tile_pool(name="keep", bufs=1))
         work = ctx.enter_context(tc.tile_pool(name="work", bufs=4))
+        slots = ctx.enter_context(tc.tile_pool(name="slots", bufs=GBUFS))
         psum = ctx.enter_context(tc.psum_pool(name="psum", bufs=3))
         psum_y = ctx.enter_context(tc.psum_pool(name="psum_y", bufs=2))
 
@@ -55,26 +59,17 @@ def tile_moe_cap2_glu_gelu_kernel(tc, xT, w1, w3, w2, gate, offs, pos1, pos2, ou
         r1, r3, r2 = [], [], []
         gates = [keep.tile([P, T], F32, name=f"gate{c}") for c in range(2)]
         w2v = w2.rearrange("e (p j) n -> p e j n", j=4)
-
-        def load_w2(pair):
-            c = keep.tile([P, 2, 4, N], F32, name=f"r2_{pair}")
-            nc.sync.dma_start(c[:], w2v[:, 2 * pair : 2 * pair + 2])
-            r2.append(c)
-
-        for e in range(E):
-            a = keep.tile([P, 4, H], F32, name=f"r1_{e}")
-            nc.sync.dma_start(a[:], w1[e].rearrange("(p j) i -> p j i", j=4))
-            w3e = w3[e].rearrange("(p j) i -> p j i", j=4)
-            parts = []
-            for lo, hi in CUTS3[e]:
-                b = keep.tile([P, 4, 4 * (hi - lo)], F32, name=f"r3_{e}_{lo}")
-                nc.sync.dma_start(b[:], w3e[:, :, 4 * lo : 4 * hi])
-                parts.append(b)
-            r1.append([a])
-            r3.append(parts)
-            for pair in range(2):
-                if W2_LOAD[pair] == e:
-                    load_w2(pair)
+        for e in range(E + 1):
+            for group, at in zip(W2_GROUPS, W2_LOAD):
+                if at == e:
+                    c = keep.tile([P, len(group), 4, N], F32, name=f"r2_{group[0]}")
+                    nc.sync.dma_start(c[:], w2v[:, group[0] : group[-1] + 1])
+                    r2.append(c)
+            for w, raws, tag in ((w1, r1, "r1"), (w3, r3, "r3")):
+                if e < E:
+                    a = keep.tile([P, 4, H], F32, name=f"{tag}_{e}")
+                    nc.sync.dma_start(a[:], w[e].rearrange("(p j) i -> p j i", j=4))
+                    raws.append(a)
         nc.sync.dma_start(pos1_t[:], pos1)
         nc.sync.dma_start(pos2_t[:], pos2)
         for c in range(2):
@@ -91,6 +86,9 @@ def tile_moe_cap2_glu_gelu_kernel(tc, xT, w1, w3, w2, gate, offs, pos1, pos2, ou
         dummy2 = keep.tile([P, 1], F32, name="dummy2")
         nc.scalar.activation(out=dummy2[:], in_=dummy[:], func=GELU)
 
+        def quantize(words, scales, values):
+            nc.vector.quantize_mx(out=words.bitcast(FP8X4), scales=scales, in_=values)
+
         xb = keep.tile([P, T, 4], BF16, name="xb", align_bytes=64)
 
         def turn(engine_copy, dst, src):
@@ -103,56 +101,49 @@ def tile_moe_cap2_glu_gelu_kernel(tc, xT, w1, w3, w2, gate, offs, pos1, pos2, ou
         for (width, s_cols), xc in zip(XCH, xr):
             if s_cols:
                 turn(nc.scalar.copy, xb[:, lo : lo + s_cols, :], xc[:, :, 0:s_cols])
-            if s_cols < width:
-                turn(nc.vector.tensor_copy, xb[:, lo + s_cols : lo + width, :], xc[:, :, s_cols:width])
-            nc.vector.quantize_mx(
-                out=xq[:, lo : lo + width].bitcast(FP8X4),
-                scales=xs[:, lo : lo + width],
-                in_=xb[:, lo : lo + width, :].rearrange("p t j -> p (t j)"),
-            )
-            lo += width
+            turn(nc.vector.tensor_copy, xb[:, lo + s_cols : lo + width, :], xc[:, :, s_cols:width])
+            hi = lo + width
+            while lo < hi:
+                q = lo + max(n for n in (128, 256, 512) if n <= hi - lo)
+                quantize(xq[:, lo:q], xs[:, lo:q], xb[:, lo:q, :].rearrange("p t j -> p (t j)"))
+                lo = q
 
-        def prepare(raws, tag, cuts, shares):
+        def cast(raw, tag, share):
             wb = work.tile([P, 4, P, 4], BF16, name=tag + "b", align_bytes=64)
+            for copy, c0, c1 in ((nc.scalar.copy, 0, share), (nc.vector.tensor_copy, share, P)):
+                if c0 < c1:
+                    copy(
+                        out=wb[:, :, c0:c1, :].rearrange("p (u v) m j -> p u m j v", v=2),
+                        in_=raw[:, :, 4 * c0 : 4 * c1].rearrange("p j (m u v) -> p u m j v", u=2, v=2),
+                    )
+            return wb
+
+        def quantize_weights(wb, tag):
             wq = work.tile([P, 4, P], U32, name=tag + "q", align_bytes=64)
             ws = work.tile([P, 4, P], U8, name=tag + "s", align_bytes=64)
-            for raw, (lo, hi), share in zip(raws, cuts, shares):
-                for copy, c0, c1 in ((nc.scalar.copy, lo, lo + share), (nc.vector.tensor_copy, lo + share, hi)):
-                    if c0 < c1:
-                        copy(
-                            out=wb[:, :, c0:c1, :].rearrange("p (u v) m j -> p u m j v", v=2),
-                            in_=raw[:, :, 4 * (c0 - lo) : 4 * (c1 - lo)].rearrange("p j (m u v) -> p u m j v", u=2, v=2),
-                        )
-                if hi - lo == P:
-                    nc.vector.quantize_mx(
-                        out=wq[:].rearrange("p t m -> p (t m)").bitcast(FP8X4),
-                        scales=ws[:].rearrange("p t m -> p (t m)"),
-                        in_=wb[:].rearrange("p t m j -> p (t m j)"),
-                    )
-                else:
-                    for t in range(4):
-                        nc.vector.quantize_mx(
-                            out=wq[:, t, lo:hi].bitcast(FP8X4),
-                            scales=ws[:, t, lo:hi],
-                            in_=wb[:, t, lo:hi, :].rearrange("p m j -> p (m j)"),
-                        )
+            quantize(
+                wq[:].rearrange("p t m -> p (t m)"),
+                ws[:].rearrange("p t m -> p (t m)"),
+                wb[:].rearrange("p t m j -> p (t m j)"),
+            )
             return wq, ws
 
         def gather(e, count):
-            xgw = work.tile([P, count * C], U32, name="xgw", align_bytes=64)
-            xgs = work.tile([P, count * C], U8, name="xgs", align_bytes=64)
+            xgw = slots.tile([P, count * C], U32, name="xgw", align_bytes=64)
+            xgs = slots.tile([P, count * C], U8, name="xgs", align_bytes=64)
             cols = slice(e * C // 16, (e + count) * C // 16)
             nc.vector.tensor_copy(xgw[:], xq[:].bitcast(U32).indirect(offs_t[:, cols]))
             nc.vector.tensor_copy(xgs[:], xs[:].indirect(offs_t[:, cols]))
             return [(xgw[:, i * C : (i + 1) * C], xgs[:, i * C : (i + 1) * C]) for i in range(count)]
 
+        halves = (slice(0, P), slice(P, C))
+
         def project(weights, tokens, tag):
             wq, ws = weights
             xgw, xgs = tokens
             banks = []
-            for half in range(2):
+            for sl in halves:
                 acc = psum.tile([P, 4, P], F32, name=tag)
-                sl = slice(half * P, (half + 1) * P)
                 for t in range(4):
                     nc.tensor.matmul_mx(
                         out=acc[:, t, :],
@@ -166,16 +157,38 @@ def tile_moe_cap2_glu_gelu_kernel(tc, xT, w1, w3, w2, gate, offs, pos1, pos2, ou
                 banks.append(acc)
             return banks
 
-        def prepare_w2(pair):
-            w2b = work.tile([P, 2, N, 4], BF16, name="w2b", align_bytes=64)
-            w2q = work.tile([P, 2 * N], U32, name="w2q", align_bytes=64)
-            w2s = work.tile([P, 2 * N], U8, name="w2s", align_bytes=64)
-            for i in range(2):
-                turn(nc.scalar.copy if i < W2S[pair] else nc.vector.tensor_copy, w2b[:, i], r2[pair][:, i])
-            nc.vector.quantize_mx(
-                out=w2q[:].bitcast(FP8X4), scales=w2s[:], in_=w2b[:].rearrange("p e n j -> p (e n j)")
+        def activate(banks):
+            gs = []
+            for bank in banks:
+                g = work.tile([P, P, 4], F32, name="g")
+                nc.scalar.activation(out=g[:], in_=bank[:].rearrange("p t n -> p n t"), func=GELU)
+                gs.append(g)
+            return gs
+
+        def multiply(hb, half, gs, banks):
+            nc.vector.tensor_tensor(
+                out=hb[:, halves[half], :], in0=gs[half][:], in1=banks[half][:].rearrange("p t n -> p n t"), op=MULT
             )
-            return [(w2q[:, i * N : (i + 1) * N], w2s[:, i * N : (i + 1) * N]) for i in range(2)]
+
+        def quantize_hidden(hb, pieces):
+            hq = work.tile([P, C], U32, name="hq", align_bytes=64)
+            hs = work.tile([P, C], U8, name="hs", align_bytes=64)
+            for sl in pieces:
+                quantize(hq[:, sl], hs[:, sl], hb[:, sl, :].rearrange("p n j -> p (n j)"))
+            return hq, hs
+
+        def cast_w2(pair):
+            group = W2_GROUPS[pair]
+            w2b = work.tile([P, len(group), N, 4], BF16, name="w2b", align_bytes=64)
+            for i, f in enumerate(group):
+                turn(nc.scalar.copy if W2_S[f] else nc.vector.tensor_copy, w2b[:, i], r2[pair][:, i])
+            return w2b, len(group)
+
+        def quantize_w2(w2b, count):
+            w2q = work.tile([P, count * N], U32, name="w2q", align_bytes=64)
+            w2s = work.tile([P, count * N], U8, name="w2s", align_bytes=64)
+            quantize(w2q[:], w2s[:], w2b[:].rearrange("p e n j -> p (e n j)"))
+            return [(w2q[:, i * N : (i + 1) * N], w2s[:, i * N : (i + 1) * N]) for i in range(count)]
 
         def finish(acc, weights, hidden, pieces):
             w2q, w2s = weights
@@ -191,52 +204,64 @@ def tile_moe_cap2_glu_gelu_kernel(tc, xT, w1, w3, w2, gate, offs, pos1, pos2, ou
                     stop=True,
                 )
 
-        halves = (slice(0, P), slice(P, C))
         whole = (slice(0, C),)
         hidden = []
-        w2qs = {}
         tokens = {}
-        tokens[0], tokens[1] = gather(0, 2)
+        before = None
+        w2qs = []
         for e in range(E):
-            if e == 1:
-                tokens[2], tokens[3] = gather(2, 2)
-            banks_a = project(prepare(r1[e], "w1", ((0, P),), (MS1[e],)), tokens[e], "acc_a")
-            w3qs = prepare(r3[e], "w3", CUTS3[e], MS3[e])
-            gs = []
-            for half in range(2):
-                g = work.tile([P, P, 4], F32, name="g")
-                nc.scalar.activation(out=g[:], in_=banks_a[half][:].rearrange("p t n -> p n t"), func=GELU)
-                gs.append(g)
+            for pair, at in enumerate(W2_LOAD):
+                if at == e:
+                    w2qs = w2qs + quantize_w2(*cast_w2(pair))
+            for group in GROUPS:
+                if group[0] == e:
+                    for f, got in zip(group, gather(e, len(group))):
+                        tokens[f] = got
+            if before and not LAG[e - 1]:
+                multiply(before[0], 0, before[1], before[2])
+                multiply(before[0], 1, before[1], before[2])
+            wb1 = cast(r1[e], "w1", S1[e])
+            if before and LAG[e - 1]:
+                multiply(before[0], 0, before[1], before[2])
+            if before and LAG[e - 1] == 2:
+                multiply(before[0], 1, before[1], before[2])
+            if before and not LAG[e - 1]:
+                hidden.append(quantize_hidden(before[0], whole))
+            banks_a = project(quantize_weights(wb1, "w1"), tokens[e], "acc_a")
+            if before and LAG[e - 1] == 2:
+                hidden.append(quantize_hidden(before[0], whole))
+            wb3 = cast(r3[e], "w3", S3[e])
+            gs = activate(banks_a)
+            if before and LAG[e - 1] == 1:
+                multiply(before[0], 1, before[1], before[2])
+            w3qs = quantize_weights(wb3, "w3")
+            if before and LAG[e - 1] == 1:
+                hidden.append(quantize_hidden(before[0], whole))
             banks_b = project(w3qs, tokens[e], "acc_b")
-            for pair in range(2):
-                if W2_AT[pair] == e:
-                    w2qs[2 * pair], w2qs[2 * pair + 1] = prepare_w2(pair)
             hb = work.tile([P, C, 4], BF16, name="hb", align_bytes=64)
-            hq = work.tile([P, C], U32, name="hq", align_bytes=64)
-            hs = work.tile([P, C], U8, name="hs", align_bytes=64)
-            for half in range(2):
-                nc.vector.tensor_tensor(
-                    out=hb[:, halves[half], :], in0=gs[half][:], in1=banks_b[half][:].rearrange("p t n -> p n t"), op=MULT
-                )
-            pieces = halves if e == E - 1 else whole
-            for sl in pieces:
-                nc.vector.quantize_mx(
-                    out=hq[:, sl].bitcast(FP8X4), scales=hs[:, sl], in_=hb[:, sl, :].rearrange("p n j -> p (n j)")
-                )
-            hidden.append((hq, hs))
-            for group in Y_GROUPS:
-                if e == Y_AT[group]:
-                    y = psum_y.tile([P, 2 * C], F32, name="y")
-                    for i, f in enumerate(group):
-                        finish(y[:, i * C : (i + 1) * C], w2qs[f], hidden[f], halves if f == E - 1 else whole)
-                    lo = group[0] * C
-                    hi = lo + len(group) * C
-                    cut = lo + P if e == E - 1 and group == (E - 1,) else hi
-                    nc.scalar.copy(out=ys[:, lo:cut], in_=y[:, 0 : cut - lo])
-                    if cut < hi:
-                        nc.scalar.copy(out=ys[:, cut:hi], in_=y[:, cut - lo : hi - lo])
+            before = (hb, gs, banks_b)
 
-        cuts = (0, 448, T)
+        late = [cast_w2(pair) for pair, at in enumerate(W2_LOAD) if at == E]
+        multiply(before[0], 0, before[1], before[2])
+        for w2b in late[:-1]:
+            w2qs = w2qs + quantize_w2(*w2b)
+        multiply(before[0], 1, before[1], before[2])
+        for w2b in late[-1:]:
+            w2qs = w2qs + quantize_w2(*w2b)
+        hidden.append(quantize_hidden(before[0], halves))
+        for group in Y_GROUPS:
+            y = psum_y.tile([P, 2 * C], F32, name="y")
+            for i, f in enumerate(group):
+                finish(y[:, i * C : (i + 1) * C], w2qs[f], hidden[f], (slice(0, C),))
+            lo = group[0] * C
+            nc.scalar.copy(out=ys[:, lo : lo + len(group) * C], in_=y[:, 0 : len(group) * C])
+        for half, sl in enumerate(halves):
+            y = psum_y.tile([P, 2 * C], F32, name="y")
+            finish(y, w2qs[E - 1], hidden[E - 1], (sl,))
+            lo = (E - 1) * C
+            (nc.vector.tensor_copy if YV and half else nc.scalar.copy)(out=ys[:, lo + sl.start : lo + sl.stop], in_=y[:, sl])
+
+        cuts = (0, CUT, T)
         toks = [slice(cuts[i], cuts[i + 1]) for i in range(2)]
         z1 = keep.tile([P, T], F32, name="z1")
         nc.vector.tensor_tensor(z1[:], ys[:].indirect(pos1_t[:]), gates[0][:], MULT)

@@ -19,18 +19,20 @@ S = E * C
 PAD = 32
 WIN = 704
 FLOPS = 2 * S * K * H * 2 + 2 * S * H * N
-S1 = (128, 40, 40, 64)
-S3 = (128, 88, 88, 64)
+S1 = (128, 72, 72, 80)
+S3 = (128, 64, 64, 64)
 GROUPS = ((0, 1), (2, 3))
 GBUFS = 2
 W2_GROUPS = ((0,), (1,), (2,), (3,))
 W2_LOAD = (4, 4, 4, 4)
 W2_S = (1, 0, 1, 1)
-LAG = (0, 0, 0)
-YV = 0
+YV = 1
+GMODE = 1
+VORD = 0
+HQ_HOLD = (0, 0, 0)
 Y_GROUPS = ((0, 1), (2,))
-CUT = 384
-XCH = ((384, 128), (256, 96))
+CUT = 320
+XCH = ((640, 256),)
 
 
 def tile_moe_cap2_glu_gelu_kernel(tc, xT, w1, w3, w2, gate, offs, pos1, pos2, out):
@@ -108,15 +110,12 @@ def tile_moe_cap2_glu_gelu_kernel(tc, xT, w1, w3, w2, gate, offs, pos1, pos2, ou
                 quantize(xq[:, lo:q], xs[:, lo:q], xb[:, lo:q, :].rearrange("p t j -> p (t j)"))
                 lo = q
 
-        def cast(raw, tag, share):
-            wb = work.tile([P, 4, P, 4], BF16, name=tag + "b", align_bytes=64)
-            for copy, c0, c1 in ((nc.scalar.copy, 0, share), (nc.vector.tensor_copy, share, P)):
-                if c0 < c1:
-                    copy(
-                        out=wb[:, :, c0:c1, :].rearrange("p (u v) m j -> p u m j v", v=2),
-                        in_=raw[:, :, 4 * c0 : 4 * c1].rearrange("p j (m u v) -> p u m j v", u=2, v=2),
-                    )
-            return wb
+        def cast(copy, wb, raw, c0, c1):
+            if c0 < c1:
+                copy(
+                    out=wb[:, :, c0:c1, :].rearrange("p (u v) m j -> p u m j v", v=2),
+                    in_=raw[:, :, 4 * c0 : 4 * c1].rearrange("p j (m u v) -> p u m j v", u=2, v=2),
+                )
 
         def quantize_weights(wb, tag):
             wq = work.tile([P, 4, P], U32, name=tag + "q", align_bytes=64)
@@ -157,21 +156,28 @@ def tile_moe_cap2_glu_gelu_kernel(tc, xT, w1, w3, w2, gate, offs, pos1, pos2, ou
                 banks.append(acc)
             return banks
 
-        def activate(banks):
+        def activate(banks, raw, tag):
+            if GMODE == 0:
+                room = keep.tile([P, 4, 2 * P], F32, name="g", tag=tag)
+            else:
+                room = raw
             gs = []
-            for bank in banks:
-                g = work.tile([P, P, 4], F32, name="g")
-                nc.scalar.activation(out=g[:], in_=bank[:].rearrange("p t n -> p n t"), func=GELU)
+            for half, bank in enumerate(banks):
+                g = room[:, :, half * P : (half + 1) * P].rearrange("p a (n t) -> p a n t", t=4)
+                nc.scalar.activation(out=g, in_=bank[:].rearrange("p t (a n) -> p a n t", a=4), func=GELU)
                 gs.append(g)
             return gs
 
         def multiply(hb, half, gs, banks):
             nc.vector.tensor_tensor(
-                out=hb[:, halves[half], :], in0=gs[half][:], in1=banks[half][:].rearrange("p t n -> p n t"), op=MULT
+                out=hb[:, halves[half], :].rearrange("p (a n) t -> p a n t", a=4),
+                in0=gs[half],
+                in1=banks[half][:].rearrange("p t (a n) -> p a n t", a=4),
+                op=MULT,
             )
 
-        def quantize_hidden(hb, pieces):
-            hq = work.tile([P, C], U32, name="hq", align_bytes=64)
+        def quantize_hidden(hb, pieces, tag):
+            hq = keep.tile([P, C], U32, name="hq", tag=tag, align_bytes=64)
             hs = work.tile([P, C], U8, name="hs", align_bytes=64)
             for sl in pieces:
                 quantize(hq[:, sl], hs[:, sl], hb[:, sl, :].rearrange("p n j -> p (n j)"))
@@ -207,48 +213,50 @@ def tile_moe_cap2_glu_gelu_kernel(tc, xT, w1, w3, w2, gate, offs, pos1, pos2, ou
         whole = (slice(0, C),)
         hidden = []
         tokens = {}
-        before = None
-        w2qs = []
+        for group in GROUPS:
+            for f, got in zip(group, gather(group[0], len(group))):
+                tokens[f] = got
+        banks_a = banks_b = None
         for e in range(E):
-            for pair, at in enumerate(W2_LOAD):
-                if at == e:
-                    w2qs = w2qs + quantize_w2(*cast_w2(pair))
-            for group in GROUPS:
-                if group[0] == e:
-                    for f, got in zip(group, gather(e, len(group))):
-                        tokens[f] = got
-            if before and not LAG[e - 1]:
-                multiply(before[0], 0, before[1], before[2])
-                multiply(before[0], 1, before[1], before[2])
-            wb1 = cast(r1[e], "w1", S1[e])
-            if before and LAG[e - 1]:
-                multiply(before[0], 0, before[1], before[2])
-            if before and LAG[e - 1] == 2:
-                multiply(before[0], 1, before[1], before[2])
-            if before and not LAG[e - 1]:
-                hidden.append(quantize_hidden(before[0], whole))
-            banks_a = project(quantize_weights(wb1, "w1"), tokens[e], "acc_a")
-            if before and LAG[e - 1] == 2:
-                hidden.append(quantize_hidden(before[0], whole))
-            wb3 = cast(r3[e], "w3", S3[e])
-            gs = activate(banks_a)
-            if before and LAG[e - 1] == 1:
-                multiply(before[0], 1, before[1], before[2])
-            w3qs = quantize_weights(wb3, "w3")
-            if before and LAG[e - 1] == 1:
-                hidden.append(quantize_hidden(before[0], whole))
-            banks_b = project(w3qs, tokens[e], "acc_b")
-            hb = work.tile([P, C, 4], BF16, name="hb", align_bytes=64)
-            before = (hb, gs, banks_b)
+            wb1 = keep.tile([P, 4, P, 4], BF16, name="w1b", tag=f"w1b{e}", align_bytes=64)
+            cast(nc.scalar.copy, wb1, r1[e], 0, S1[e])
+            if VORD != 1:
+                cast(nc.vector.tensor_copy, wb1, r1[e], S1[e], P)
+            if e:
+                gs = activate(banks_a, r1[e], f"r1_{e}")
+                hb = work.tile([P, C, 4], BF16, name="hb", align_bytes=64)
+                if VORD != 3:
+                    multiply(hb, 0, gs, banks_b)
+                if VORD < 2:
+                    multiply(hb, 1, gs, banks_b)
+                if VORD < 2 and not HQ_HOLD[e - 1]:
+                    hidden.append(quantize_hidden(hb, whole, f"hq{e}"))
+            if VORD == 1:
+                cast(nc.vector.tensor_copy, wb1, r1[e], S1[e], P)
+            w1qs = quantize_weights(wb1, "w1")
+            if e:
+                if VORD == 3:
+                    multiply(hb, 0, gs, banks_b)
+                if VORD >= 2:
+                    multiply(hb, 1, gs, banks_b)
+                if VORD >= 2 or HQ_HOLD[e - 1]:
+                    hidden.append(quantize_hidden(hb, whole, f"w1b{e}" if HQ_HOLD[e - 1] else f"hq{e}"))
+            banks_a = project(w1qs, tokens[e], "acc_a")
+            wb3 = work.tile([P, 4, P, 4], BF16, name="w3b", align_bytes=64)
+            cast(nc.scalar.copy, wb3, r3[e], 0, S3[e])
+            cast(nc.vector.tensor_copy, wb3, r3[e], S3[e], P)
+            banks_b = project(quantize_weights(wb3, "w3"), tokens[e], "acc_b")
 
-        late = [cast_w2(pair) for pair, at in enumerate(W2_LOAD) if at == E]
-        multiply(before[0], 0, before[1], before[2])
+        gs = activate(banks_a, r3[E - 1], f"r3_{E - 1}")
+        hb = work.tile([P, C, 4], BF16, name="hb", align_bytes=64)
+        late = [cast_w2(pair) for pair in range(len(W2_GROUPS))]
+        w2qs = []
+        multiply(hb, 0, gs, banks_b)
         for w2b in late[:-1]:
             w2qs = w2qs + quantize_w2(*w2b)
-        multiply(before[0], 1, before[1], before[2])
-        for w2b in late[-1:]:
-            w2qs = w2qs + quantize_w2(*w2b)
-        hidden.append(quantize_hidden(before[0], halves))
+        multiply(hb, 1, gs, banks_b)
+        w2qs = w2qs + quantize_w2(*late[-1])
+        hidden.append(quantize_hidden(hb, halves, "hq"))
         for group in Y_GROUPS:
             y = psum_y.tile([P, 2 * C], F32, name="y")
             for i, f in enumerate(group):

@@ -19,20 +19,29 @@ S = E * C
 PAD = 32
 WIN = 704
 FLOPS = 2 * S * K * H * 2 + 2 * S * H * N
-S1 = (128, 72, 72, 80)
-S3 = (128, 64, 64, 64)
+SS = (128, 128, 72, 72, 72, 72, 64, 72)
+HOLD = ((2, 2), (2, 2), (2, 2), (1, 1))
+PB = 4
+HG = -1
+HB = -1
 GROUPS = ((0, 1), (2, 3))
 GBUFS = 2
 W2_GROUPS = ((0,), (1,), (2,), (3,))
 W2_LOAD = (4, 4, 4, 4)
-W2_S = (1, 0, 1, 1)
+W2_S = (1, 1, 0, 1)
 YV = 1
-GMODE = 1
-VORD = 0
-HQ_HOLD = (0, 0, 0)
-Y_GROUPS = ((0, 1), (2,))
+GMODE = 0
+G1 = (0, 0, 0, 0)
+G3 = (0, 0, 0, 0)
+GH = (1, 1, 1, 1)
+VORD = 1
+HQ_HOLD = (1, 1, 0)
+Y_GROUPS = ((0,), (1,), (2,))
 CUT = 320
-XCH = ((640, 256),)
+XL = ((0, T),)
+XS = ((0, 256),)
+XV = ((256, 512), (512, T))
+XQ = ((256, 512), (512, T), (0, 256))
 
 
 def tile_moe_cap2_glu_gelu_kernel(tc, xT, w1, w3, w2, gate, offs, pos1, pos2, out):
@@ -42,7 +51,7 @@ def tile_moe_cap2_glu_gelu_kernel(tc, xT, w1, w3, w2, gate, offs, pos1, pos2, ou
         keep = ctx.enter_context(tc.tile_pool(name="keep", bufs=1))
         work = ctx.enter_context(tc.tile_pool(name="work", bufs=4))
         slots = ctx.enter_context(tc.tile_pool(name="slots", bufs=GBUFS))
-        psum = ctx.enter_context(tc.psum_pool(name="psum", bufs=3))
+        psum = ctx.enter_context(tc.psum_pool(name="psum", bufs=PB))
         psum_y = ctx.enter_context(tc.psum_pool(name="psum_y", bufs=2))
 
         offs_t = lists.tile([P, S // 16], U16, name="offs_t")
@@ -51,12 +60,10 @@ def tile_moe_cap2_glu_gelu_kernel(tc, xT, w1, w3, w2, gate, offs, pos1, pos2, ou
 
         xv = xT.rearrange("(p j) t -> p j t", j=4)
         xr = []
-        lo = 0
-        for width, s_cols in XCH:
-            xc = keep.tile([P, 4, width], F32, name=f"x{lo}")
-            nc.sync.dma_start(xc[:], xv[:, :, lo : lo + width])
+        for lo, hi in XL:
+            xc = keep.tile([P, 4, hi - lo], F32, name=f"x{lo}")
+            nc.sync.dma_start(xc[:], xv[:, :, lo:hi])
             xr.append(xc)
-            lo += width
         nc.sync.dma_start(offs_t[:], offs)
         r1, r3, r2 = [], [], []
         gates = [keep.tile([P, T], F32, name=f"gate{c}") for c in range(2)]
@@ -99,16 +106,26 @@ def tile_moe_cap2_glu_gelu_kernel(tc, xT, w1, w3, w2, gate, offs, pos1, pos2, ou
                 in_=src.rearrange("p j (c i) -> p c j i", i=4),
             )
 
-        lo = 0
-        for (width, s_cols), xc in zip(XCH, xr):
-            if s_cols:
-                turn(nc.scalar.copy, xb[:, lo : lo + s_cols, :], xc[:, :, 0:s_cols])
-            turn(nc.vector.tensor_copy, xb[:, lo + s_cols : lo + width, :], xc[:, :, s_cols:width])
-            hi = lo + width
-            while lo < hi:
-                q = lo + max(n for n in (128, 256, 512) if n <= hi - lo)
-                quantize(xq[:, lo:q], xs[:, lo:q], xb[:, lo:q, :].rearrange("p t j -> p (t j)"))
-                lo = q
+        def x_raw(lo, hi):
+            for (c0, c1), xc in zip(XL, xr):
+                if c0 <= lo and hi <= c1:
+                    return xc[:, :, lo - c0 : hi - c0]
+
+        for lo, hi in XS:
+            turn(nc.scalar.copy, xb[:, lo:hi, :], x_raw(lo, hi))
+        for lo, hi in XV:
+            turn(nc.vector.tensor_copy, xb[:, lo:hi, :], x_raw(lo, hi))
+        for lo, hi in XQ:
+            quantize(xq[:, lo:hi], xs[:, lo:hi], xb[:, lo:hi, :].rearrange("p t j -> p (t j)"))
+
+        def pool_cast(out, in_):
+            for u in range(2):
+                nc.gpsimd.tensor_scalar(out[:, u], in_[:, u], 1.0, 0.0, MULT, ADD)
+
+        def pool_turn(dst, src):
+            nc.gpsimd.tensor_scalar(
+                dst.rearrange("p (c i) j -> p c j i", i=4), src.rearrange("p j (c i) -> p c j i", i=4), 1.0, 0.0, MULT, ADD
+            )
 
         def cast(copy, wb, raw, c0, c1):
             if c0 < c1:
@@ -127,13 +144,12 @@ def tile_moe_cap2_glu_gelu_kernel(tc, xT, w1, w3, w2, gate, offs, pos1, pos2, ou
             )
             return wq, ws
 
-        def gather(e, count):
-            xgw = slots.tile([P, count * C], U32, name="xgw", align_bytes=64)
-            xgs = slots.tile([P, count * C], U8, name="xgs", align_bytes=64)
-            cols = slice(e * C // 16, (e + count) * C // 16)
-            nc.vector.tensor_copy(xgw[:], xq[:].bitcast(U32).indirect(offs_t[:, cols]))
-            nc.vector.tensor_copy(xgs[:], xs[:].indirect(offs_t[:, cols]))
-            return [(xgw[:, i * C : (i + 1) * C], xgs[:, i * C : (i + 1) * C]) for i in range(count)]
+        def gather(window, dtype, name, group, tag):
+            got = keep.tile([P, len(group) * C], dtype, name=name, tag=tag, align_bytes=64)
+            cols = slice(group[0] * C // 16, (group[-1] + 1) * C // 16)
+            nc.vector.tensor_copy(got[:], window.indirect(offs_t[:, cols]))
+            for i, f in enumerate(group):
+                tokens[f, name] = got[:, i * C : (i + 1) * C]
 
         halves = (slice(0, P), slice(P, C))
 
@@ -156,9 +172,9 @@ def tile_moe_cap2_glu_gelu_kernel(tc, xT, w1, w3, w2, gate, offs, pos1, pos2, ou
                 banks.append(acc)
             return banks
 
-        def activate(banks, raw, tag):
-            if GMODE == 0:
-                room = keep.tile([P, 4, 2 * P], F32, name="g", tag=tag)
+        def activate(banks, raw, held):
+            if not held:
+                room = work.tile([P, 4, 2 * P], F32, name="g")
             else:
                 room = raw
             gs = []
@@ -187,7 +203,10 @@ def tile_moe_cap2_glu_gelu_kernel(tc, xT, w1, w3, w2, gate, offs, pos1, pos2, ou
             group = W2_GROUPS[pair]
             w2b = work.tile([P, len(group), N, 4], BF16, name="w2b", align_bytes=64)
             for i, f in enumerate(group):
-                turn(nc.scalar.copy if W2_S[f] else nc.vector.tensor_copy, w2b[:, i], r2[pair][:, i])
+                if W2_S[f] == 2:
+                    pool_turn(w2b[:, i], r2[pair][:, i])
+                else:
+                    turn(nc.scalar.copy if W2_S[f] else nc.vector.tensor_copy, w2b[:, i], r2[pair][:, i])
             return w2b, len(group)
 
         def quantize_w2(w2b, count):
@@ -214,43 +233,71 @@ def tile_moe_cap2_glu_gelu_kernel(tc, xT, w1, w3, w2, gate, offs, pos1, pos2, ou
         hidden = []
         tokens = {}
         for group in GROUPS:
-            for f, got in zip(group, gather(group[0], len(group))):
-                tokens[f] = got
-        banks_a = banks_b = None
-        for e in range(E):
-            wb1 = keep.tile([P, 4, P, 4], BF16, name="w1b", tag=f"w1b{e}", align_bytes=64)
-            cast(nc.scalar.copy, wb1, r1[e], 0, S1[e])
-            if VORD != 1:
-                cast(nc.vector.tensor_copy, wb1, r1[e], S1[e], P)
-            if e:
-                gs = activate(banks_a, r1[e], f"r1_{e}")
-                hb = work.tile([P, C, 4], BF16, name="hb", align_bytes=64)
-                if VORD != 3:
-                    multiply(hb, 0, gs, banks_b)
-                if VORD < 2:
-                    multiply(hb, 1, gs, banks_b)
-                if VORD < 2 and not HQ_HOLD[e - 1]:
-                    hidden.append(quantize_hidden(hb, whole, f"hq{e}"))
-            if VORD == 1:
-                cast(nc.vector.tensor_copy, wb1, r1[e], S1[e], P)
-            w1qs = quantize_weights(wb1, "w1")
-            if e:
-                if VORD == 3:
-                    multiply(hb, 0, gs, banks_b)
-                if VORD >= 2:
-                    multiply(hb, 1, gs, banks_b)
-                if VORD >= 2 or HQ_HOLD[e - 1]:
-                    hidden.append(quantize_hidden(hb, whole, f"w1b{e}" if HQ_HOLD[e - 1] else f"hq{e}"))
-            banks_a = project(w1qs, tokens[e], "acc_a")
-            wb3 = work.tile([P, 4, P, 4], BF16, name="w3b", align_bytes=64)
-            cast(nc.scalar.copy, wb3, r3[e], 0, S3[e])
-            cast(nc.vector.tensor_copy, wb3, r3[e], S3[e], P)
-            banks_b = project(quantize_weights(wb3, "w3"), tokens[e], "acc_b")
-
-        gs = activate(banks_a, r3[E - 1], f"r3_{E - 1}")
-        hb = work.tile([P, C, 4], BF16, name="hb", align_bytes=64)
-        late = [cast_w2(pair) for pair in range(len(W2_GROUPS))]
+            if group != GROUPS[-1] or HG < 0:
+                gather(xq[:].bitcast(U32), U32, "xgw", group, f"xgw{group[0]}")
+            if group != GROUPS[-1] or HB < 0:
+                gather(xs[:], U8, "xgs", group, f"xgs{group[0]}")
         w2qs = []
+        banks = {}
+        gs = {}
+        hbs = {}
+        done = set()
+
+        def gelu(e, half, room):
+            g = room[:, :, half * P : (half + 1) * P].rearrange("p a (n t) -> p a n t", t=4)
+            nc.scalar.activation(out=g, in_=banks[2 * e][half][:].rearrange("p t (a n) -> p a n t", a=4), func=GELU)
+            gs[e, half] = g
+
+        def products(last):
+            for e in range(last):
+                for half in range(2):
+                    if (e, half) in gs and (e, half) not in done and 2 * e + 1 in banks:
+                        if e not in hbs:
+                            hbs[e] = work.tile([P, C, 4], BF16, name="hb", align_bytes=64)
+                        multiply(hbs[e], half, {half: gs[e, half]}, banks[2 * e + 1])
+                        done.add((e, half))
+
+        def hiddens():
+            for e in range(E - 1):
+                if (e, 0) in done and (e, 1) in done and len(hidden) == e:
+                    hidden.append(quantize_hidden(hbs[e], whole, f"hq{e}"))
+
+        for step in range(2 * E):
+            e, kind = divmod(step, 2)
+            raw = (r1, r3)[kind][e]
+            tag = ("w1", "w3")[kind]
+            wb = keep.tile([P, 4, P, 4], BF16, name=tag + "b", tag=f"wb{step}", align_bytes=64)
+            cast(nc.scalar.copy, wb, raw, 0, SS[step])
+            for f in range(E):
+                for half in range(2):
+                    if HOLD[f][half] and 2 * f + HOLD[f][half] == step:
+                        gelu(f, half, raw)
+            if VORD == 0:
+                products(E - 1)
+                hiddens()
+            cast(nc.vector.tensor_copy, wb, raw, SS[step], P)
+            if VORD == 1:
+                products(E - 1)
+            wqs = quantize_weights(wb, tag)
+            if VORD == 2:
+                products(E - 1)
+            hiddens()
+            banks[step] = project(wqs, (tokens[e, "xgw"], tokens[e, "xgs"]), ("acc_a", "acc_b")[kind])
+            if step == HG:
+                gather(xq[:].bitcast(U32), U32, "xgw", GROUPS[-1], f"wb{step}")
+            if step == HB:
+                gather(xs[:], U8, "xgs", GROUPS[-1], f"wb{step}")
+            if kind == 0:
+                room = work.tile([P, 4, 2 * P], F32, name="g")
+                for half in range(2):
+                    if not HOLD[e][half]:
+                        gelu(e, half, room)
+        products(E - 1)
+        hiddens()
+        hb = work.tile([P, C, 4], BF16, name="hb", align_bytes=64)
+        gs = [gs[E - 1, 0], gs[E - 1, 1]]
+        banks_b = banks[2 * E - 1]
+        late = [cast_w2(pair) for pair, at in enumerate(W2_LOAD) if at == E]
         multiply(hb, 0, gs, banks_b)
         for w2b in late[:-1]:
             w2qs = w2qs + quantize_w2(*w2b)
@@ -258,13 +305,13 @@ def tile_moe_cap2_glu_gelu_kernel(tc, xT, w1, w3, w2, gate, offs, pos1, pos2, ou
         w2qs = w2qs + quantize_w2(*late[-1])
         hidden.append(quantize_hidden(hb, halves, "hq"))
         for group in Y_GROUPS:
-            y = psum_y.tile([P, 2 * C], F32, name="y")
+            y = psum_y.tile([P, 2 * C], F32, name="y") if PB == 3 else psum.tile([P, 2 * C], F32, name="y", tag="acc_a")
             for i, f in enumerate(group):
                 finish(y[:, i * C : (i + 1) * C], w2qs[f], hidden[f], (slice(0, C),))
             lo = group[0] * C
             nc.scalar.copy(out=ys[:, lo : lo + len(group) * C], in_=y[:, 0 : len(group) * C])
         for half, sl in enumerate(halves):
-            y = psum_y.tile([P, 2 * C], F32, name="y")
+            y = psum_y.tile([P, 2 * C], F32, name="y") if PB == 3 else psum.tile([P, 2 * C], F32, name="y", tag="acc_a")
             finish(y, w2qs[E - 1], hidden[E - 1], (sl,))
             lo = (E - 1) * C
             (nc.vector.tensor_copy if YV and half else nc.scalar.copy)(out=ys[:, lo + sl.start : lo + sl.stop], in_=y[:, sl])

@@ -19,11 +19,12 @@ S = E * C
 PAD = 32
 WIN = 704
 FLOPS = 2 * S * K * H * 2 + 2 * S * H * N
-SS = (128, 128, 72, 72, 72, 72, 64, 72)
-HOLD = ((2, 2), (2, 2), (2, 2), (1, 1))
+SS = (112, 112, 80, 80, 72, 72, 64, 72)
+HOLD = ((0, 0), (2, 2), (2, 2), (1, 1))
 PB = 4
-HG = -1
-HB = -1
+GS = (128, 128, 128, 128, 0, 24, 0, 0)
+HG = 0
+HB = 1
 GROUPS = ((0, 1), (2, 3))
 GBUFS = 2
 W2_GROUPS = ((0,), (1,), (2,), (3,))
@@ -268,6 +269,8 @@ def tile_moe_cap2_glu_gelu_kernel(tc, xT, w1, w3, w2, gate, offs, pos1, pos2, ou
             tag = ("w1", "w3")[kind]
             wb = keep.tile([P, 4, P, 4], BF16, name=tag + "b", tag=f"wb{step}", align_bytes=64)
             cast(nc.scalar.copy, wb, raw, 0, SS[step])
+            v0 = min(P, SS[step] + GS[step])
+            cast(pool_cast, wb, raw, SS[step], v0)
             for f in range(E):
                 for half in range(2):
                     if HOLD[f][half] and 2 * f + HOLD[f][half] == step:
@@ -275,7 +278,7 @@ def tile_moe_cap2_glu_gelu_kernel(tc, xT, w1, w3, w2, gate, offs, pos1, pos2, ou
             if VORD == 0:
                 products(E - 1)
                 hiddens()
-            cast(nc.vector.tensor_copy, wb, raw, SS[step], P)
+            cast(nc.vector.tensor_copy, wb, raw, v0, P)
             if VORD == 1:
                 products(E - 1)
             wqs = quantize_weights(wb, tag)

@@ -129,7 +129,12 @@ def tile_moe_cap2_glu_gelu_kernel(tc, xT, w1, w3, w2, gate, offs, pos1, pos2, ou
             )
 
         def cast(copy, wb, raw, c0, c1):
-            if c0 < c1:
+            if c0 < c1 and copy is not pool_cast:
+                copy(
+                    out=wb[:, :, c0:c1, :].rearrange("p t m (a b) -> p m a t b", b=2),
+                    in_=raw[:, :, 4 * c0 : 4 * c1].rearrange("p (a b) (m t) -> p m a t b", b=2, t=4),
+                )
+            elif c0 < c1:
                 copy(
                     out=wb[:, :, c0:c1, :].rearrange("p (u v) m j -> p u m j v", v=2),
                     in_=raw[:, :, 4 * c0 : 4 * c1].rearrange("p j (m u v) -> p u m j v", u=2, v=2),

@@ -14,35 +14,24 @@ ADD = mybir.AluOpType.add
 GELU = mybir.ActivationFunctionType.Gelu_apprx_tanh
 
 P = 128
+PACK = 4
+LIST = 16
 K, T, E, C, H, N = 512, 640, 4, 256, 512, 128
 S = E * C
 PAD = 32
-WIN = 704
+WINDOW = 704
 FLOPS = 2 * S * K * H * 2 + 2 * S * H * N
-SS = (112, 112, 80, 80, 72, 72, 64, 72)
-HOLD = ((0, 0), (2, 2), (2, 2), (1, 1))
-PB = 4
-GS = (128, 128, 128, 128, 0, 24, 0, 0)
-HG = 0
-HB = 1
-GROUPS = ((0, 1), (2, 3))
-GBUFS = 2
-W2_GROUPS = ((0,), (1,), (2,), (3,))
-W2_LOAD = (4, 4, 4, 4)
-W2_S = (1, 1, 0, 1)
-YV = 1
-GMODE = 0
-G1 = (0, 0, 0, 0)
-G3 = (0, 0, 0, 0)
-GH = (1, 1, 1, 1)
-VORD = 1
-HQ_HOLD = (1, 1, 0)
-Y_GROUPS = ((0,), (1,), (2,))
-CUT = 320
-XL = ((0, T),)
-XS = ((0, 256),)
-XV = ((256, 512), (512, T))
-XQ = ((256, 512), (512, T), (0, 256))
+HALVES = (slice(0, P), slice(P, C))
+
+X_PIECES = (slice(0, 256), slice(256, 512), slice(512, T))
+
+SHARES = (
+    ((112, 16), (112, 16)),
+    ((80, 48), (80, 48)),
+    ((72, 0), (72, 24)),
+    ((64, 0), (72, 0)),
+)
+W2_ON_VECTOR = 2
 
 
 def tile_moe_cap2_glu_gelu_kernel(tc, xT, w1, w3, w2, gate, offs, pos1, pos2, out):
@@ -50,290 +39,206 @@ def tile_moe_cap2_glu_gelu_kernel(tc, xT, w1, w3, w2, gate, offs, pos1, pos2, ou
     with ExitStack() as ctx:
         lists = ctx.enter_context(tc.tile_pool(name="lists", bufs=1))
         keep = ctx.enter_context(tc.tile_pool(name="keep", bufs=1))
-        work = ctx.enter_context(tc.tile_pool(name="work", bufs=4))
-        slots = ctx.enter_context(tc.tile_pool(name="slots", bufs=GBUFS))
-        psum = ctx.enter_context(tc.psum_pool(name="psum", bufs=PB))
-        psum_y = ctx.enter_context(tc.psum_pool(name="psum_y", bufs=2))
+        each = ctx.enter_context(tc.tile_pool(name="each", bufs=E))
+        psum = ctx.enter_context(tc.psum_pool(name="psum", bufs=4))
 
-        offs_t = lists.tile([P, S // 16], U16, name="offs_t")
-        pos1_t = lists.tile([P, T // 16], U16, name="pos1_t")
-        pos2_t = lists.tile([P, T // 16], U16, name="pos2_t")
-
-        xv = xT.rearrange("(p j) t -> p j t", j=4)
-        xr = []
-        for lo, hi in XL:
-            xc = keep.tile([P, 4, hi - lo], F32, name=f"x{lo}")
-            nc.sync.dma_start(xc[:], xv[:, :, lo:hi])
-            xr.append(xc)
+        offs_t = lists.tile([P, S // LIST], U16, name="offs_t")
+        pos1_t = lists.tile([P, T // LIST], U16, name="pos1_t")
+        pos2_t = lists.tile([P, T // LIST], U16, name="pos2_t")
+        x_raw = keep.tile([P, PACK, T], F32, name="x_raw")
+        nc.sync.dma_start(x_raw[:], xT.rearrange("(p j) t -> p j t", j=PACK))
         nc.sync.dma_start(offs_t[:], offs)
-        r1, r3, r2 = [], [], []
-        gates = [keep.tile([P, T], F32, name=f"gate{c}") for c in range(2)]
-        w2v = w2.rearrange("e (p j) n -> p e j n", j=4)
-        for e in range(E + 1):
-            for group, at in zip(W2_GROUPS, W2_LOAD):
-                if at == e:
-                    c = keep.tile([P, len(group), 4, N], F32, name=f"r2_{group[0]}")
-                    nc.sync.dma_start(c[:], w2v[:, group[0] : group[-1] + 1])
-                    r2.append(c)
-            for w, raws, tag in ((w1, r1, "r1"), (w3, r3, "r3")):
-                if e < E:
-                    a = keep.tile([P, 4, H], F32, name=f"{tag}_{e}")
-                    nc.sync.dma_start(a[:], w[e].rearrange("(p j) i -> p j i", j=4))
-                    raws.append(a)
+        w_raw = {}
+        for e in range(E):
+            for which, w in enumerate((w1, w3)):
+                w_raw[e, which] = keep.tile([P, PACK, H], F32, name=f"w_raw{e}{which}")
+                nc.sync.dma_start(w_raw[e, which][:], w[e].rearrange("(p j) i -> p j i", j=PACK))
+        w2_raw = []
+        for e in range(E):
+            w2_raw.append(keep.tile([P, PACK, N], F32, name=f"w2_raw{e}"))
+            nc.sync.dma_start(w2_raw[e][:], w2[e].rearrange("(p j) n -> p j n", j=PACK))
         nc.sync.dma_start(pos1_t[:], pos1)
         nc.sync.dma_start(pos2_t[:], pos2)
-        for c in range(2):
-            nc.sync.dma_start(gates[c][:], gate[c])
+        gates = []
+        for choice in range(2):
+            gates.append(keep.tile([P, T], F32, name=f"gate{choice}"))
+            nc.sync.dma_start(gates[choice][:], gate[choice])
 
-        xs = keep.tile([P, WIN], U8, name="xs", align_bytes=64)
-        nc.gpsimd.memset(xs[:], 0)
-        xq = keep.tile([P, WIN], I32, name="xq", align_bytes=64)
-        nc.vector.memset(xq[:, T:WIN], 0)
-        ys = keep.tile([P, S + PAD], F32, name="ys")
-        nc.vector.memset(ys[:, S : S + PAD], 0.0)
-        dummy = keep.tile([P, 1], F32, name="dummy")
-        nc.vector.memset(dummy[:], 0.0)
-        dummy2 = keep.tile([P, 1], F32, name="dummy2")
-        nc.scalar.activation(out=dummy2[:], in_=dummy[:], func=GELU)
+        x_scales = keep.tile([P, WINDOW], U8, name="x_scales", align_bytes=64)
+        nc.gpsimd.memset(x_scales[:], 0)
+        x_words = keep.tile([P, WINDOW], I32, name="x_words", align_bytes=64)
+        nc.vector.memset(x_words[:, T:WINDOW], 0)
+        results = keep.tile([P, S + PAD], F32, name="results")
+        zeros = keep.tile([P, PAD], F32, name="zeros")
+        nc.vector.memset(zeros[:], 0.0)
+        nc.scalar.activation(out=results[:, S : S + PAD], in_=zeros[:], func=GELU)
 
         def quantize(words, scales, values):
             nc.vector.quantize_mx(out=words.bitcast(FP8X4), scales=scales, in_=values)
 
-        xb = keep.tile([P, T, 4], BF16, name="xb", align_bytes=64)
-
-        def turn(engine_copy, dst, src):
-            engine_copy(
-                out=dst.rearrange("p (c i) j -> p c j i", i=4),
-                in_=src.rearrange("p j (c i) -> p c j i", i=4),
+        def product(acc, weights, moving):
+            nc.tensor.matmul_mx(
+                out=acc,
+                lhsT=weights[0].bitcast(FP8X4),
+                lhsT_scale=weights[1],
+                rhs=moving[0].bitcast(FP8X4),
+                rhs_scale=moving[1],
+                start=True,
+                stop=True,
             )
 
-        def x_raw(lo, hi):
-            for (c0, c1), xc in zip(XL, xr):
-                if c0 <= lo and hi <= c1:
-                    return xc[:, :, lo - c0 : hi - c0]
+        def interleave(copy, dst, src):
+            copy(
+                out=dst.rearrange("p (c i) j -> p c j i", i=PACK),
+                in_=src.rearrange("p j (c i) -> p c j i", i=PACK),
+            )
 
-        for lo, hi in XS:
-            turn(nc.scalar.copy, xb[:, lo:hi, :], x_raw(lo, hi))
-        for lo, hi in XV:
-            turn(nc.vector.tensor_copy, xb[:, lo:hi, :], x_raw(lo, hi))
-        for lo, hi in XQ:
-            quantize(xq[:, lo:hi], xs[:, lo:hi], xb[:, lo:hi, :].rearrange("p t j -> p (t j)"))
+        x_bf = keep.tile([P, T, PACK], BF16, name="x_bf", align_bytes=64)
+        interleave(nc.scalar.copy, x_bf[:, X_PIECES[0], :], x_raw[:, :, X_PIECES[0]])
+        for piece in X_PIECES[1:]:
+            interleave(nc.vector.tensor_copy, x_bf[:, piece, :], x_raw[:, :, piece])
+        for piece in X_PIECES[1:] + X_PIECES[:1]:
+            quantize(x_words[:, piece], x_scales[:, piece], x_bf[:, piece, :].rearrange("p t j -> p (t j)"))
 
-        def pool_cast(out, in_):
+        def gather(window, dtype, pair, tag):
+            picked = keep.tile([P, 2 * C], dtype, name="picked", tag=tag, align_bytes=64)
+            columns = slice(pair * 2 * C // LIST, (pair + 1) * 2 * C // LIST)
+            nc.vector.tensor_copy(picked[:], window.indirect(offs_t[:, columns]))
+            return [picked[:, 0:C], picked[:, C : 2 * C]]
+
+        def round_weights(copy, w_bf, raw, lo, hi):
+            copy(
+                out=w_bf[:, :, lo:hi, :].rearrange("p t m (a b) -> p m a t b", b=2),
+                in_=raw[:, :, PACK * lo : PACK * hi].rearrange("p (a b) (m t) -> p m a t b", b=2, t=PACK),
+            )
+
+        def round_weights_on_gpsimd(w_bf, raw, lo, hi):
+            dst = w_bf[:, :, lo:hi, :].rearrange("p (u v) m j -> p u m j v", v=2)
+            src = raw[:, :, PACK * lo : PACK * hi].rearrange("p j (m u v) -> p u m j v", u=2, v=2)
             for u in range(2):
-                nc.gpsimd.tensor_scalar(out[:, u], in_[:, u], 1.0, 0.0, MULT, ADD)
+                nc.gpsimd.tensor_scalar(dst[:, u], src[:, u], 1.0, 0.0, MULT, ADD)
 
-        def pool_turn(dst, src):
-            nc.gpsimd.tensor_scalar(
-                dst.rearrange("p (c i) j -> p c j i", i=4), src.rearrange("p j (c i) -> p c j i", i=4), 1.0, 0.0, MULT, ADD
-            )
-
-        def cast(copy, wb, raw, c0, c1):
-            if c0 < c1 and copy is not pool_cast:
-                copy(
-                    out=wb[:, :, c0:c1, :].rearrange("p t m (a b) -> p m a t b", b=2),
-                    in_=raw[:, :, 4 * c0 : 4 * c1].rearrange("p (a b) (m t) -> p m a t b", b=2, t=4),
-                )
-            elif c0 < c1:
-                copy(
-                    out=wb[:, :, c0:c1, :].rearrange("p (u v) m j -> p u m j v", v=2),
-                    in_=raw[:, :, 4 * c0 : 4 * c1].rearrange("p j (m u v) -> p u m j v", u=2, v=2),
-                )
-
-        def quantize_weights(wb, tag):
-            wq = work.tile([P, 4, P], U32, name=tag + "q", align_bytes=64)
-            ws = work.tile([P, 4, P], U8, name=tag + "s", align_bytes=64)
+        def quantize_weights(w_bf, tag):
+            words = each.tile([P, PACK, P], U32, name="w_words", tag=tag + "_words", align_bytes=64)
+            scales = each.tile([P, PACK, P], U8, name="w_scales", tag=tag + "_scales", align_bytes=64)
             quantize(
-                wq[:].rearrange("p t m -> p (t m)"),
-                ws[:].rearrange("p t m -> p (t m)"),
-                wb[:].rearrange("p t m j -> p (t m j)"),
+                words[:].rearrange("p t m -> p (t m)"),
+                scales[:].rearrange("p t m -> p (t m)"),
+                w_bf[:].rearrange("p t m j -> p (t m j)"),
             )
-            return wq, ws
+            return words, scales
 
-        def gather(window, dtype, name, group, tag):
-            got = keep.tile([P, len(group) * C], dtype, name=name, tag=tag, align_bytes=64)
-            cols = slice(group[0] * C // 16, (group[-1] + 1) * C // 16)
-            nc.vector.tensor_copy(got[:], window.indirect(offs_t[:, cols]))
-            for i, f in enumerate(group):
-                tokens[f, name] = got[:, i * C : (i + 1) * C]
-
-        halves = (slice(0, P), slice(P, C))
-
-        def project(weights, tokens, tag):
-            wq, ws = weights
-            xgw, xgs = tokens
+        def project(weights, e, tag):
             banks = []
-            for sl in halves:
-                acc = psum.tile([P, 4, P], F32, name=tag)
-                for t in range(4):
-                    nc.tensor.matmul_mx(
-                        out=acc[:, t, :],
-                        lhsT=wq[:, t, :].bitcast(FP8X4),
-                        lhsT_scale=ws[:, t, :],
-                        rhs=xgw[:, sl].bitcast(FP8X4),
-                        rhs_scale=xgs[:, sl],
-                        start=True,
-                        stop=True,
+            for half in HALVES:
+                acc = psum.tile([P, PACK, P], F32, name="acc", tag=tag)
+                for t in range(PACK):
+                    product(
+                        acc[:, t, :],
+                        (weights[0][:, t, :], weights[1][:, t, :]),
+                        (slot_words[e][:, half], slot_scales[e][:, half]),
                     )
                 banks.append(acc)
             return banks
 
-        def activate(banks, raw, held):
-            if not held:
-                room = work.tile([P, 4, 2 * P], F32, name="g")
-            else:
-                room = raw
-            gs = []
-            for half, bank in enumerate(banks):
-                g = room[:, :, half * P : (half + 1) * P].rearrange("p a (n t) -> p a n t", t=4)
-                nc.scalar.activation(out=g, in_=bank[:].rearrange("p t (a n) -> p a n t", a=4), func=GELU)
-                gs.append(g)
-            return gs
+        def by_slot(bank):
+            return bank[:].rearrange("p t (r n) -> p r n t", r=PACK)
 
-        def multiply(hb, half, gs, banks):
+        def gelu(banks, room):
+            gelus = []
+            for i, bank in enumerate(banks):
+                gelus.append(room[:, :, i * P : (i + 1) * P].rearrange("p r (n t) -> p r n t", t=PACK))
+                nc.scalar.activation(out=gelus[i], in_=by_slot(bank), func=GELU)
+            return gelus
+
+        def multiply(h_bf, i, gelus, banks):
             nc.vector.tensor_tensor(
-                out=hb[:, halves[half], :].rearrange("p (a n) t -> p a n t", a=4),
-                in0=gs[half],
-                in1=banks[half][:].rearrange("p t (a n) -> p a n t", a=4),
+                out=h_bf[:, HALVES[i], :].rearrange("p (r n) t -> p r n t", r=PACK),
+                in0=gelus[i],
+                in1=by_slot(banks[i]),
                 op=MULT,
             )
 
-        def quantize_hidden(hb, pieces, tag):
-            hq = keep.tile([P, C], U32, name="hq", tag=tag, align_bytes=64)
-            hs = work.tile([P, C], U8, name="hs", align_bytes=64)
-            for sl in pieces:
-                quantize(hq[:, sl], hs[:, sl], hb[:, sl, :].rearrange("p n j -> p (n j)"))
-            return hq, hs
+        def quantize_hidden(h_bf, pieces):
+            words = each.tile([P, C], U32, name="h_words", align_bytes=64)
+            scales = each.tile([P, C], U8, name="h_scales", align_bytes=64)
+            for piece in pieces:
+                quantize(words[:, piece], scales[:, piece], h_bf[:, piece, :].rearrange("p n t -> p (n t)"))
+            return words, scales
 
-        def cast_w2(pair):
-            group = W2_GROUPS[pair]
-            w2b = work.tile([P, len(group), N, 4], BF16, name="w2b", align_bytes=64)
-            for i, f in enumerate(group):
-                if W2_S[f] == 2:
-                    pool_turn(w2b[:, i], r2[pair][:, i])
-                else:
-                    turn(nc.scalar.copy if W2_S[f] else nc.vector.tensor_copy, w2b[:, i], r2[pair][:, i])
-            return w2b, len(group)
+        def first_layer(e, which, waiting):
+            raw = w_raw[e, which]
+            on_scalar, on_gpsimd = SHARES[e][which]
+            w_bf = keep.tile([P, PACK, P, PACK], BF16, name="w_bf", tag=f"w_bf{e}{which}", align_bytes=64)
+            round_weights(nc.scalar.copy, w_bf, raw, 0, on_scalar)
+            if on_gpsimd:
+                round_weights_on_gpsimd(w_bf, raw, on_scalar, on_scalar + on_gpsimd)
+            gelus = gelu(waiting, raw) if waiting else None
+            if on_scalar + on_gpsimd < P:
+                round_weights(nc.vector.tensor_copy, w_bf, raw, on_scalar + on_gpsimd, P)
+            return w_bf, gelus
 
-        def quantize_w2(w2b, count):
-            w2q = work.tile([P, count * N], U32, name="w2q", align_bytes=64)
-            w2s = work.tile([P, count * N], U8, name="w2s", align_bytes=64)
-            quantize(w2q[:], w2s[:], w2b[:].rearrange("p e n j -> p (e n j)"))
-            return [(w2q[:, i * N : (i + 1) * N], w2s[:, i * N : (i + 1) * N]) for i in range(count)]
-
-        def finish(acc, weights, hidden, pieces):
-            w2q, w2s = weights
-            hq, hs = hidden
-            for sl in pieces:
-                nc.tensor.matmul_mx(
-                    out=acc[:, sl],
-                    lhsT=w2q.bitcast(FP8X4),
-                    lhsT_scale=w2s,
-                    rhs=hq[:, sl].bitcast(FP8X4),
-                    rhs_scale=hs[:, sl],
-                    start=True,
-                    stop=True,
-                )
-
-        whole = (slice(0, C),)
+        slot_words = gather(x_words[:].bitcast(U32), U32, 0, "words01")
+        slot_scales = gather(x_scales[:], U8, 0, "scales01")
+        last = E - 1
         hidden = []
-        tokens = {}
-        for group in GROUPS:
-            if group != GROUPS[-1] or HG < 0:
-                gather(xq[:].bitcast(U32), U32, "xgw", group, f"xgw{group[0]}")
-            if group != GROUPS[-1] or HB < 0:
-                gather(xs[:], U8, "xgs", group, f"xgs{group[0]}")
-        w2qs = []
-        banks = {}
-        gs = {}
-        hbs = {}
-        done = set()
+        sums1 = sums3 = gelus = None
+        for e in range(E):
+            w_bf, waited = first_layer(e, 0, sums1 if e > 1 else None)
+            if e > 0:
+                h_bf = each.tile([P, C, PACK], BF16, name="h_bf", align_bytes=64)
+                for i in range(2):
+                    multiply(h_bf, i, waited or gelus, sums3)
+            weights = quantize_weights(w_bf, "w1")
+            if e > 0:
+                hidden.append(quantize_hidden(h_bf, [slice(0, C)]))
+            sums1 = project(weights, e, "sums1")
+            if e == 0:
+                slot_words = slot_words + gather(x_words[:].bitcast(U32), U32, 1, "w_bf00")
+                room = keep.tile([P, PACK, C], F32, name="room")
+                gelus = gelu(sums1, room)
+            w_bf, waited = first_layer(e, 1, sums1 if e == last else None)
+            sums3 = project(quantize_weights(w_bf, "w3"), e, "sums3")
+            if e == 0:
+                slot_scales = slot_scales + gather(x_scales[:], U8, 1, "w_bf01")
 
-        def gelu(e, half, room):
-            g = room[:, :, half * P : (half + 1) * P].rearrange("p a (n t) -> p a n t", t=4)
-            nc.scalar.activation(out=g, in_=banks[2 * e][half][:].rearrange("p t (a n) -> p a n t", a=4), func=GELU)
-            gs[e, half] = g
+        w2_bf = []
+        for e in range(E):
+            w2_bf.append(each.tile([P, N, PACK], BF16, name="w2_bf", align_bytes=64))
+            interleave(nc.vector.tensor_copy if e == W2_ON_VECTOR else nc.scalar.copy, w2_bf[e][:], w2_raw[e][:])
 
-        def products(last):
-            for e in range(last):
-                for half in range(2):
-                    if (e, half) in gs and (e, half) not in done and 2 * e + 1 in banks:
-                        if e not in hbs:
-                            hbs[e] = work.tile([P, C, 4], BF16, name="hb", align_bytes=64)
-                        multiply(hbs[e], half, {half: gs[e, half]}, banks[2 * e + 1])
-                        done.add((e, half))
+        def quantize_w2(e):
+            words = each.tile([P, N], U32, name="w2_words", align_bytes=64)
+            scales = each.tile([P, N], U8, name="w2_scales", align_bytes=64)
+            quantize(words[:], scales[:], w2_bf[e][:].rearrange("p n j -> p (n j)"))
+            return words[:], scales[:]
 
-        def hiddens():
-            for e in range(E - 1):
-                if (e, 0) in done and (e, 1) in done and len(hidden) == e:
-                    hidden.append(quantize_hidden(hbs[e], whole, f"hq{e}"))
+        h_bf = each.tile([P, C, PACK], BF16, name="h_bf", align_bytes=64)
+        multiply(h_bf, 0, waited, sums3)
+        w2_mx = [quantize_w2(e) for e in range(last)]
+        multiply(h_bf, 1, waited, sums3)
+        w2_mx.append(quantize_w2(last))
+        hidden.append(quantize_hidden(h_bf, HALVES))
 
-        for step in range(2 * E):
-            e, kind = divmod(step, 2)
-            raw = (r1, r3)[kind][e]
-            tag = ("w1", "w3")[kind]
-            wb = keep.tile([P, 4, P, 4], BF16, name=tag + "b", tag=f"wb{step}", align_bytes=64)
-            cast(nc.scalar.copy, wb, raw, 0, SS[step])
-            v0 = min(P, SS[step] + GS[step])
-            cast(pool_cast, wb, raw, SS[step], v0)
-            for f in range(E):
-                for half in range(2):
-                    if HOLD[f][half] and 2 * f + HOLD[f][half] == step:
-                        gelu(f, half, raw)
-            if VORD == 0:
-                products(E - 1)
-                hiddens()
-            cast(nc.vector.tensor_copy, wb, raw, v0, P)
-            if VORD == 1:
-                products(E - 1)
-            wqs = quantize_weights(wb, tag)
-            if VORD == 2:
-                products(E - 1)
-            hiddens()
-            banks[step] = project(wqs, (tokens[e, "xgw"], tokens[e, "xgs"]), ("acc_a", "acc_b")[kind])
-            if step == HG:
-                gather(xq[:].bitcast(U32), U32, "xgw", GROUPS[-1], f"wb{step}")
-            if step == HB:
-                gather(xs[:], U8, "xgs", GROUPS[-1], f"wb{step}")
-            if kind == 0:
-                room = work.tile([P, 4, 2 * P], F32, name="g")
-                for half in range(2):
-                    if not HOLD[e][half]:
-                        gelu(e, half, room)
-        products(E - 1)
-        hiddens()
-        hb = work.tile([P, C, 4], BF16, name="hb", align_bytes=64)
-        gs = [gs[E - 1, 0], gs[E - 1, 1]]
-        banks_b = banks[2 * E - 1]
-        late = [cast_w2(pair) for pair, at in enumerate(W2_LOAD) if at == E]
-        multiply(hb, 0, gs, banks_b)
-        for w2b in late[:-1]:
-            w2qs = w2qs + quantize_w2(*w2b)
-        multiply(hb, 1, gs, banks_b)
-        w2qs = w2qs + quantize_w2(*late[-1])
-        hidden.append(quantize_hidden(hb, halves, "hq"))
-        for group in Y_GROUPS:
-            y = psum_y.tile([P, 2 * C], F32, name="y") if PB == 3 else psum.tile([P, 2 * C], F32, name="y", tag="acc_a")
-            for i, f in enumerate(group):
-                finish(y[:, i * C : (i + 1) * C], w2qs[f], hidden[f], (slice(0, C),))
-            lo = group[0] * C
-            nc.scalar.copy(out=ys[:, lo : lo + len(group) * C], in_=y[:, 0 : len(group) * C])
-        for half, sl in enumerate(halves):
-            y = psum_y.tile([P, 2 * C], F32, name="y") if PB == 3 else psum.tile([P, 2 * C], F32, name="y", tag="acc_a")
-            finish(y, w2qs[E - 1], hidden[E - 1], (sl,))
-            lo = (E - 1) * C
-            (nc.vector.tensor_copy if YV and half else nc.scalar.copy)(out=ys[:, lo + sl.start : lo + sl.stop], in_=y[:, sl])
+        def second_layer(e, piece, copy):
+            acc = psum.tile([P, C], F32, name="acc", tag="sums1")
+            product(acc[:, piece], w2_mx[e], (hidden[e][0][:, piece], hidden[e][1][:, piece]))
+            copy(out=results[:, e * C + piece.start : e * C + piece.stop], in_=acc[:, piece])
 
-        cuts = (0, CUT, T)
-        toks = [slice(cuts[i], cuts[i + 1]) for i in range(2)]
-        z1 = keep.tile([P, T], F32, name="z1")
-        nc.vector.tensor_tensor(z1[:], ys[:].indirect(pos1_t[:]), gates[0][:], MULT)
-        z2 = []
-        for i in range(2):
-            z2.append(keep.tile([P, cuts[i + 1] - cuts[i]], F32, name=f"z2_{i}"))
-            cols = slice(cuts[i] // 16, cuts[i + 1] // 16)
-            nc.vector.tensor_tensor(z2[i][:], ys[:].indirect(pos2_t[:, cols]), gates[1][:, toks[i]], MULT)
-        for i in range(2):
-            total = keep.tile([P, cuts[i + 1] - cuts[i]], F32, name=f"total{i}")
-            nc.vector.tensor_tensor(total[:], z1[:, toks[i]], z2[i][:], ADD)
-            nc.sync.dma_start(out[:, toks[i]], total[:])
+        for e in range(last):
+            second_layer(e, slice(0, C), nc.scalar.copy)
+        second_layer(last, HALVES[0], nc.scalar.copy)
+        second_layer(last, HALVES[1], nc.vector.tensor_copy)
+
+        first = keep.tile([P, T], F32, name="first")
+        nc.vector.tensor_tensor(first[:], results[:].indirect(pos1_t[:]), gates[0][:], MULT)
+        token_halves = (slice(0, T // 2), slice(T // 2, T))
+        second = []
+        for i, tokens in enumerate(token_halves):
+            second.append(keep.tile([P, T // 2], F32, name=f"second{i}"))
+            columns = slice(tokens.start // LIST, tokens.stop // LIST)
+            nc.vector.tensor_tensor(second[i][:], results[:].indirect(pos2_t[:, columns]), gates[1][:, tokens], MULT)
+        for i, tokens in enumerate(token_halves):
+            total = keep.tile([P, T // 2], F32, name=f"total{i}")
+            nc.vector.tensor_tensor(total[:], first[:, tokens], second[i][:], ADD)
+            nc.sync.dma_start(out[:, tokens], total[:])

@@ -25,13 +25,9 @@ HALVES = (slice(0, P), slice(P, C))
 
 X_PIECES = (slice(0, 256), slice(256, 512), slice(512, T))
 
-SHARES = (
-    ((112, 16), (112, 16)),
-    ((80, 48), (80, 48)),
-    ((72, 0), (72, 24)),
-    ((64, 0), (72, 0)),
-)
-W2_ON_VECTOR = 2
+W1_ON_SCALAR = (72, 72, 72, 72)
+W3_ON_SCALAR = (40, 40, 40, 40)
+PAIRS = 2
 
 
 def tile_moe_cap2_glu_gelu_kernel(tc, xT, w1, w3, w2, gate, offs, pos1, pos2, out):
@@ -54,9 +50,9 @@ def tile_moe_cap2_glu_gelu_kernel(tc, xT, w1, w3, w2, gate, offs, pos1, pos2, ou
                 w_raw[e, which] = keep.tile([P, PACK, H], F32, name=f"w_raw{e}{which}")
                 nc.sync.dma_start(w_raw[e, which][:], w[e].rearrange("(p j) i -> p j i", j=PACK))
         w2_raw = []
-        for e in range(E):
-            w2_raw.append(keep.tile([P, PACK, N], F32, name=f"w2_raw{e}"))
-            nc.sync.dma_start(w2_raw[e][:], w2[e].rearrange("(p j) n -> p j n", j=PACK))
+        for pair in range(2):
+            w2_raw.append(keep.tile([P, 2, PACK, N], F32, name=f"w2_raw{pair}"))
+            nc.sync.dma_start(w2_raw[pair][:], w2[2 * pair : 2 * pair + 2].rearrange("e (p j) n -> p e j n", j=PACK))
         nc.sync.dma_start(pos1_t[:], pos1)
         nc.sync.dma_start(pos2_t[:], pos2)
         gates = []
@@ -93,51 +89,46 @@ def tile_moe_cap2_glu_gelu_kernel(tc, xT, w1, w3, w2, gate, offs, pos1, pos2, ou
                 in_=src.rearrange("p j (c i) -> p c j i", i=PACK),
             )
 
-        x_bf = keep.tile([P, T, PACK], BF16, name="x_bf", align_bytes=64)
+        x_bf = keep.tile([P, T, PACK], BF16, name="x_bf", tag="before_w1_0", align_bytes=64)
         interleave(nc.scalar.copy, x_bf[:, X_PIECES[0], :], x_raw[:, :, X_PIECES[0]])
         for piece in X_PIECES[1:]:
             interleave(nc.vector.tensor_copy, x_bf[:, piece, :], x_raw[:, :, piece])
         for piece in X_PIECES[1:] + X_PIECES[:1]:
             quantize(x_words[:, piece], x_scales[:, piece], x_bf[:, piece, :].rearrange("p t j -> p (t j)"))
 
-        def gather(window, dtype, pair, tag):
-            picked = keep.tile([P, 2 * C], dtype, name="picked", tag=tag, align_bytes=64)
-            columns = slice(pair * 2 * C // LIST, (pair + 1) * 2 * C // LIST)
+        def gather(window, dtype, first, count, tag):
+            picked = keep.tile([P, count * C], dtype, name="picked", tag=tag, align_bytes=64)
+            columns = slice(first * C // LIST, (first + count) * C // LIST)
             nc.vector.tensor_copy(picked[:], window.indirect(offs_t[:, columns]))
-            return [picked[:, 0:C], picked[:, C : 2 * C]]
+            return [picked[:, i * C : (i + 1) * C] for i in range(count)]
 
-        def round_weights(copy, w_bf, raw, lo, hi):
-            copy(
-                out=w_bf[:, :, lo:hi, :].rearrange("p t m (a b) -> p m a t b", b=2),
-                in_=raw[:, :, PACK * lo : PACK * hi].rearrange("p (a b) (m t) -> p m a t b", b=2, t=PACK),
-            )
+        def round_weights(copy, w_bf, raw, u, lo, hi):
+            src = raw[:, :, PACK * lo : PACK * hi].rearrange("p (a b) (m u v) -> p u m a v b", b=2, u=PAIRS, v=2)
+            copy(out=w_bf[:, :, lo:hi, :].rearrange("p v m (a b) -> p m a v b", b=2), in_=src[:, u])
 
-        def round_weights_on_gpsimd(w_bf, raw, lo, hi):
-            dst = w_bf[:, :, lo:hi, :].rearrange("p (u v) m j -> p u m j v", v=2)
-            src = raw[:, :, PACK * lo : PACK * hi].rearrange("p j (m u v) -> p u m j v", u=2, v=2)
-            for u in range(2):
-                nc.gpsimd.tensor_scalar(dst[:, u], src[:, u], 1.0, 0.0, MULT, ADD)
+        def round_weights_on_gpsimd(w_bf, raw, u, lo, hi):
+            src = raw[:, :, PACK * lo : PACK * hi].rearrange("p j (m u v) -> p u m v j", u=PAIRS, v=2)
+            nc.gpsimd.tensor_scalar(w_bf[:, :, lo:hi, :].rearrange("p v m j -> p m v j"), src[:, u], 1.0, 0.0, MULT, ADD)
 
         def quantize_weights(w_bf, tag):
-            words = each.tile([P, PACK, P], U32, name="w_words", tag=tag + "_words", align_bytes=64)
-            scales = each.tile([P, PACK, P], U8, name="w_scales", tag=tag + "_scales", align_bytes=64)
-            quantize(
-                words[:].rearrange("p t m -> p (t m)"),
-                scales[:].rearrange("p t m -> p (t m)"),
-                w_bf[:].rearrange("p t m j -> p (t m j)"),
-            )
-            return words, scales
+            weights = []
+            for u in range(PAIRS):
+                words = each.tile([P, 2, P], U32, name="w_words", tag=f"{tag}_words{u}", align_bytes=64)
+                scales = each.tile([P, 2, P], U8, name="w_scales", tag=f"{tag}_scales{u}", align_bytes=64)
+                quantize(
+                    words[:].rearrange("p v m -> p (v m)"),
+                    scales[:].rearrange("p v m -> p (v m)"),
+                    w_bf[u][:].rearrange("p v m j -> p (v m j)"),
+                )
+                weights.extend((words[:, v, :], scales[:, v, :]) for v in range(2))
+            return weights
 
         def project(weights, e, tag):
             banks = []
             for half in HALVES:
                 acc = psum.tile([P, PACK, P], F32, name="acc", tag=tag)
                 for t in range(PACK):
-                    product(
-                        acc[:, t, :],
-                        (weights[0][:, t, :], weights[1][:, t, :]),
-                        (slot_words[e][:, half], slot_scales[e][:, half]),
-                    )
+                    product(acc[:, t, :], weights[t], (slot_words[e][:, half], slot_scales[e][:, half]))
                 banks.append(acc)
             return banks
 
@@ -153,72 +144,84 @@ def tile_moe_cap2_glu_gelu_kernel(tc, xT, w1, w3, w2, gate, offs, pos1, pos2, ou
 
         def multiply(h_bf, i, gelus, banks):
             nc.vector.tensor_tensor(
-                out=h_bf[:, HALVES[i], :].rearrange("p (r n) t -> p r n t", r=PACK),
+                out=h_bf[i][:].rearrange("p (r n) t -> p r n t", r=PACK),
                 in0=gelus[i],
                 in1=by_slot(banks[i]),
                 op=MULT,
             )
 
-        def quantize_hidden(h_bf, pieces):
-            words = each.tile([P, C], U32, name="h_words", align_bytes=64)
+        def hidden_tiles(e):
+            return [keep.tile([P, P, PACK], BF16, name="h_bf", tag=f"h_bf{e}{i}", align_bytes=64) for i in range(2)]
+
+        def quantize_hidden(h_bf, tag):
+            words = keep.tile([P, C], U32, name="h_words", tag=tag, align_bytes=64)
             scales = each.tile([P, C], U8, name="h_scales", align_bytes=64)
-            for piece in pieces:
-                quantize(words[:, piece], scales[:, piece], h_bf[:, piece, :].rearrange("p n t -> p (n t)"))
+            for i, half in enumerate(HALVES):
+                quantize(words[:, half], scales[:, half], h_bf[i][:].rearrange("p n t -> p (n t)"))
             return words, scales
 
-        def first_layer(e, which, waiting):
-            raw = w_raw[e, which]
-            on_scalar, on_gpsimd = SHARES[e][which]
-            w_bf = keep.tile([P, PACK, P, PACK], BF16, name="w_bf", tag=f"w_bf{e}{which}", align_bytes=64)
-            round_weights(nc.scalar.copy, w_bf, raw, 0, on_scalar)
-            if on_gpsimd:
-                round_weights_on_gpsimd(w_bf, raw, on_scalar, on_scalar + on_gpsimd)
-            gelus = gelu(waiting, raw) if waiting else None
-            if on_scalar + on_gpsimd < P:
-                round_weights(nc.vector.tensor_copy, w_bf, raw, on_scalar + on_gpsimd, P)
-            return w_bf, gelus
+        def rounded_tiles(tags):
+            return [keep.tile([P, 2, P, PACK], BF16, name="w_bf", tag=tag, align_bytes=64) for tag in tags]
 
-        slot_words = gather(x_words[:].bitcast(U32), U32, 0, "words01")
-        slot_scales = gather(x_scales[:], U8, 0, "scales01")
+        def round_w1(e):
+            w_bf = rounded_tiles([f"w1_bf{e}", f"before_w1_{e}"])
+            split = 2 * W1_ON_SCALAR[e] - P
+            round_weights(nc.scalar.copy, w_bf[0], w_raw[e, 0], 0, 0, P)
+            if split:
+                round_weights(nc.scalar.copy, w_bf[1], w_raw[e, 0], 1, 0, split)
+            if split < P:
+                round_weights_on_gpsimd(w_bf[1], w_raw[e, 0], 1, split, P)
+            return w_bf
+
+        def round_w3(e):
+            w_bf = rounded_tiles([f"w3_bf{e}", f"before_w1_{e + 1}"])
+            for u in range(PAIRS):
+                round_weights(nc.scalar.copy, w_bf[u], w_raw[e, 1], u, 0, W3_ON_SCALAR[e])
+                round_weights(nc.vector.tensor_copy, w_bf[u], w_raw[e, 1], u, W3_ON_SCALAR[e], P)
+            return w_bf
+
+        x_word_window = x_words[:].bitcast(U32)
+        slot_words = gather(x_word_window, U32, 0, 2, "words01")
+        slot_scales = gather(x_scales[:], U8, 0, 2, "scales01")
         last = E - 1
         hidden = []
-        sums1 = sums3 = gelus = None
+        sums3 = gelus = None
         for e in range(E):
-            w_bf, waited = first_layer(e, 0, sums1 if e > 1 else None)
+            w_bf = round_w1(e)
             if e > 0:
-                h_bf = each.tile([P, C, PACK], BF16, name="h_bf", align_bytes=64)
+                h_bf = hidden_tiles(e - 1)
                 for i in range(2):
-                    multiply(h_bf, i, waited or gelus, sums3)
-            weights = quantize_weights(w_bf, "w1")
-            if e > 0:
-                hidden.append(quantize_hidden(h_bf, [slice(0, C)]))
-            sums1 = project(weights, e, "sums1")
-            if e == 0:
-                slot_words = slot_words + gather(x_words[:].bitcast(U32), U32, 1, "w_bf00")
-                room = keep.tile([P, PACK, C], F32, name="room")
-                gelus = gelu(sums1, room)
-            w_bf, waited = first_layer(e, 1, sums1 if e == last else None)
+                    multiply(h_bf, i, gelus, sums3)
+            sums1 = project(quantize_weights(w_bf, "w1"), e, "sums1")
+            w_bf = round_w3(e)
+            gelus = gelu(sums1, w_raw[e, 1])
             sums3 = project(quantize_weights(w_bf, "w3"), e, "sums3")
             if e == 0:
-                slot_scales = slot_scales + gather(x_scales[:], U8, 1, "w_bf01")
+                slot_words = slot_words + gather(x_word_window, U32, 2, 2, "w3_bf0")
+            else:
+                hidden.append(quantize_hidden(h_bf, f"w3_bf{e}"))
+            if 0 < e < last:
+                slot_scales = slot_scales + gather(x_scales[:], U8, e + 1, 1, f"h_bf{e - 1}0")
 
         w2_bf = []
-        for e in range(E):
-            w2_bf.append(each.tile([P, N, PACK], BF16, name="w2_bf", align_bytes=64))
-            interleave(nc.vector.tensor_copy if e == W2_ON_VECTOR else nc.scalar.copy, w2_bf[e][:], w2_raw[e][:])
+        for pair, (copy, tag) in enumerate(((nc.vector.tensor_copy, f"before_w1_{E}"), (nc.scalar.copy, "w2_bf"))):
+            both = keep.tile([P, 2, N, PACK], BF16, name="w2_bf", tag=tag, align_bytes=64)
+            for i in range(2):
+                interleave(copy, both[:, i], w2_raw[pair][:, i])
+                w2_bf.append(both[:, i])
 
         def quantize_w2(e):
             words = each.tile([P, N], U32, name="w2_words", align_bytes=64)
             scales = each.tile([P, N], U8, name="w2_scales", align_bytes=64)
-            quantize(words[:], scales[:], w2_bf[e][:].rearrange("p n j -> p (n j)"))
+            quantize(words[:], scales[:], w2_bf[e].rearrange("p n j -> p (n j)"))
             return words[:], scales[:]
 
-        h_bf = each.tile([P, C, PACK], BF16, name="h_bf", align_bytes=64)
-        multiply(h_bf, 0, waited, sums3)
+        h_bf = hidden_tiles(last)
+        multiply(h_bf, 0, gelus, sums3)
         w2_mx = [quantize_w2(e) for e in range(last)]
-        multiply(h_bf, 1, waited, sums3)
+        multiply(h_bf, 1, gelus, sums3)
         w2_mx.append(quantize_w2(last))
-        hidden.append(quantize_hidden(h_bf, HALVES))
+        hidden.append(quantize_hidden(h_bf, "h_words_last"))
 
         def second_layer(e, piece, copy):
             acc = psum.tile([P, C], F32, name="acc", tag="sums1")

@@ -25,9 +25,13 @@ HALVES = (slice(0, P), slice(P, C))
 
 X_PIECES = (slice(0, 256), slice(256, 512), slice(512, T))
 
-W1_ON_SCALAR = (72, 72, 72, 72)
-W3_ON_SCALAR = (40, 40, 40, 40)
+W1_ON_SCALAR = 24
+W3_ON_SCALAR = (64, 64, 64, 56)
+RAW_BYTES = PACK * H * 4
+GELU_AT, WORDS_AT, OTHER_AT = 0, 4096, 5120
 PAIRS = 2
+W2_ORDER = (0, 1, 2, 3)
+W2_ON_VECTOR = 1
 
 
 def tile_moe_cap2_glu_gelu_kernel(tc, xT, w1, w3, w2, gate, offs, pos1, pos2, out):
@@ -35,8 +39,9 @@ def tile_moe_cap2_glu_gelu_kernel(tc, xT, w1, w3, w2, gate, offs, pos1, pos2, ou
     with ExitStack() as ctx:
         lists = ctx.enter_context(tc.tile_pool(name="lists", bufs=1))
         keep = ctx.enter_context(tc.tile_pool(name="keep", bufs=1))
+        reused = ctx.enter_context(tc.tile_pool(name="reused", bufs=1))
         each = ctx.enter_context(tc.tile_pool(name="each", bufs=E))
-        psum = ctx.enter_context(tc.psum_pool(name="psum", bufs=4))
+        psum = ctx.enter_context(tc.psum_pool(name="psum", bufs=1))
 
         offs_t = lists.tile([P, S // LIST], U16, name="offs_t")
         pos1_t = lists.tile([P, T // LIST], U16, name="pos1_t")
@@ -47,12 +52,15 @@ def tile_moe_cap2_glu_gelu_kernel(tc, xT, w1, w3, w2, gate, offs, pos1, pos2, ou
         w_raw = {}
         for e in range(E):
             for which, w in enumerate((w1, w3)):
-                w_raw[e, which] = keep.tile([P, PACK, H], F32, name=f"w_raw{e}{which}")
+                if which == 0:
+                    w_raw[e, which] = keep.tile([P, PACK, H], F32, name=f"w1_raw{e}")
+                else:
+                    w_raw[e, which] = reused.tile([P, PACK, H], F32, name=f"w3_raw{e}", offset=RAW_BYTES * e)
                 nc.sync.dma_start(w_raw[e, which][:], w[e].rearrange("(p j) i -> p j i", j=PACK))
-        w2_raw = []
-        for pair in range(2):
-            w2_raw.append(keep.tile([P, 2, PACK, N], F32, name=f"w2_raw{pair}"))
-            nc.sync.dma_start(w2_raw[pair][:], w2[2 * pair : 2 * pair + 2].rearrange("e (p j) n -> p e j n", j=PACK))
+        w2_raw = {}
+        for e in W2_ORDER:
+            w2_raw[e] = keep.tile([P, PACK, N], F32, name=f"w2_raw{e}")
+            nc.sync.dma_start(w2_raw[e][:], w2[e].rearrange("(p j) n -> p j n", j=PACK))
         nc.sync.dma_start(pos1_t[:], pos1)
         nc.sync.dma_start(pos2_t[:], pos2)
         gates = []
@@ -89,45 +97,62 @@ def tile_moe_cap2_glu_gelu_kernel(tc, xT, w1, w3, w2, gate, offs, pos1, pos2, ou
                 in_=src.rearrange("p j (c i) -> p c j i", i=PACK),
             )
 
-        x_bf = keep.tile([P, T, PACK], BF16, name="x_bf", tag="before_w1_0", align_bytes=64)
+        x_bf = keep.tile([P, T, PACK], BF16, name="x_bf", tag="w1_bf0", align_bytes=64)
         interleave(nc.scalar.copy, x_bf[:, X_PIECES[0], :], x_raw[:, :, X_PIECES[0]])
         for piece in X_PIECES[1:]:
             interleave(nc.vector.tensor_copy, x_bf[:, piece, :], x_raw[:, :, piece])
         for piece in X_PIECES[1:] + X_PIECES[:1]:
             quantize(x_words[:, piece], x_scales[:, piece], x_bf[:, piece, :].rearrange("p t j -> p (t j)"))
 
-        def gather(window, dtype, first, count, tag):
-            picked = keep.tile([P, count * C], dtype, name="picked", tag=tag, align_bytes=64)
+        def gather(window, dtype, first, count, name, offset=None):
+            pool = keep if offset is None else reused
+            picked = pool.tile([P, count * C], dtype, name=name, align_bytes=64, offset=offset)
             columns = slice(first * C // LIST, (first + count) * C // LIST)
             nc.vector.tensor_copy(picked[:], window.indirect(offs_t[:, columns]))
             return [picked[:, i * C : (i + 1) * C] for i in range(count)]
 
-        def round_weights(copy, w_bf, raw, u, lo, hi):
+        def pair_tiles(tags):
+            return [keep.tile([P, 2, P, PACK], BF16, name="w_bf", tag=tag, align_bytes=64) for tag in tags]
+
+        def round_pair(copy, pairs, raw, u, lo, hi):
             src = raw[:, :, PACK * lo : PACK * hi].rearrange("p (a b) (m u v) -> p u m a v b", b=2, u=PAIRS, v=2)
-            copy(out=w_bf[:, :, lo:hi, :].rearrange("p v m (a b) -> p m a v b", b=2), in_=src[:, u])
+            copy(out=pairs[u][:, :, lo:hi, :].rearrange("p v m (a b) -> p m a v b", b=2), in_=src[:, u])
 
-        def round_weights_on_gpsimd(w_bf, raw, u, lo, hi):
-            src = raw[:, :, PACK * lo : PACK * hi].rearrange("p j (m u v) -> p u m v j", u=PAIRS, v=2)
-            nc.gpsimd.tensor_scalar(w_bf[:, :, lo:hi, :].rearrange("p v m j -> p m v j"), src[:, u], 1.0, 0.0, MULT, ADD)
+        def round_w1(e):
+            raw, split = w_raw[e, 0], W1_ON_SCALAR
+            pairs = pair_tiles([f"w1_bf{e}0", f"w1_bf{e}"])
+            round_pair(nc.scalar.copy, pairs, raw, 0, 0, P)
+            round_pair(nc.scalar.copy, pairs, raw, 1, 0, split)
+            src = raw[:, :, PACK * split : H].rearrange("p j (m u v) -> p u m v j", u=PAIRS, v=2)
+            nc.gpsimd.tensor_scalar(pairs[1][:, :, split:P, :].rearrange("p v m j -> p m v j"), src[:, 1], 1.0, 0.0, MULT, ADD)
+            return pairs
 
-        def quantize_weights(w_bf, tag):
+        def round_w3(e):
+            pairs = pair_tiles([f"w3_bf{e}0", "w1_bf1" if e == 0 else f"w3_bf{e}1"])
+            for copy, lo, hi in ((nc.scalar.copy, 0, W3_ON_SCALAR[e]), (nc.vector.tensor_copy, W3_ON_SCALAR[e], P)):
+                for u in range(PAIRS):
+                    round_pair(copy, pairs, w_raw[e, 1], u, lo, hi)
+            return pairs
+
+        def quantize_weights(parts, tag):
             weights = []
-            for u in range(PAIRS):
-                words = each.tile([P, 2, P], U32, name="w_words", tag=f"{tag}_words{u}", align_bytes=64)
-                scales = each.tile([P, 2, P], U8, name="w_scales", tag=f"{tag}_scales{u}", align_bytes=64)
+            for u, w_bf in enumerate(parts):
+                tiles = w_bf.shape[1]
+                words = each.tile([P, tiles, P], U32, name="w_words", tag=f"{tag}_words{u}", align_bytes=64)
+                scales = each.tile([P, tiles, P], U8, name="w_scales", tag=f"{tag}_scales{u}", align_bytes=64)
                 quantize(
-                    words[:].rearrange("p v m -> p (v m)"),
-                    scales[:].rearrange("p v m -> p (v m)"),
-                    w_bf[u][:].rearrange("p v m j -> p (v m j)"),
+                    words[:].rearrange("p t m -> p (t m)"),
+                    scales[:].rearrange("p t m -> p (t m)"),
+                    w_bf[:].rearrange("p t m j -> p (t m j)"),
                 )
-                weights.extend((words[:, v, :], scales[:, v, :]) for v in range(2))
+                weights.extend((words[:, t, :], scales[:, t, :]) for t in range(tiles))
             return weights
 
-        def project(weights, e, tag):
+        def project(weights, e, tags):
             banks = []
-            for half in HALVES:
+            for half, tag in zip(HALVES, tags):
                 acc = psum.tile([P, PACK, P], F32, name="acc", tag=tag)
-                for t in range(PACK):
+                for t in range(PACK) if half.start == 0 else (2, 3, 0, 1):
                     product(acc[:, t, :], weights[t], (slot_words[e][:, half], slot_scales[e][:, half]))
                 banks.append(acc)
             return banks
@@ -144,41 +169,23 @@ def tile_moe_cap2_glu_gelu_kernel(tc, xT, w1, w3, w2, gate, offs, pos1, pos2, ou
 
         def multiply(h_bf, i, gelus, banks):
             nc.vector.tensor_tensor(
-                out=h_bf[i][:].rearrange("p (r n) t -> p r n t", r=PACK),
+                out=h_bf[:, HALVES[i], :].rearrange("p (r n) t -> p r n t", r=PACK),
                 in0=gelus[i],
                 in1=by_slot(banks[i]),
                 op=MULT,
             )
 
-        def hidden_tiles(e):
-            return [keep.tile([P, P, PACK], BF16, name="h_bf", tag=f"h_bf{e}{i}", align_bytes=64) for i in range(2)]
+        def hidden_tile(e):
+            return keep.tile([P, C, PACK], BF16, name="h_bf", tag=f"w1_bf{e + 2}", align_bytes=64)
 
-        def quantize_hidden(h_bf, tag):
-            words = keep.tile([P, C], U32, name="h_words", tag=tag, align_bytes=64)
+        def quantize_hidden(h_bf, pieces, words):
             scales = each.tile([P, C], U8, name="h_scales", align_bytes=64)
-            for i, half in enumerate(HALVES):
-                quantize(words[:, half], scales[:, half], h_bf[i][:].rearrange("p n t -> p (n t)"))
+            for piece in pieces:
+                quantize(words[:, piece], scales[:, piece], h_bf[:, piece, :].rearrange("p n t -> p (n t)"))
             return words, scales
 
-        def rounded_tiles(tags):
-            return [keep.tile([P, 2, P, PACK], BF16, name="w_bf", tag=tag, align_bytes=64) for tag in tags]
-
-        def round_w1(e):
-            w_bf = rounded_tiles([f"w1_bf{e}", f"before_w1_{e}"])
-            split = 2 * W1_ON_SCALAR[e] - P
-            round_weights(nc.scalar.copy, w_bf[0], w_raw[e, 0], 0, 0, P)
-            if split:
-                round_weights(nc.scalar.copy, w_bf[1], w_raw[e, 0], 1, 0, split)
-            if split < P:
-                round_weights_on_gpsimd(w_bf[1], w_raw[e, 0], 1, split, P)
-            return w_bf
-
-        def round_w3(e):
-            w_bf = rounded_tiles([f"w3_bf{e}", f"before_w1_{e + 1}"])
-            for u in range(PAIRS):
-                round_weights(nc.scalar.copy, w_bf[u], w_raw[e, 1], u, 0, W3_ON_SCALAR[e])
-                round_weights(nc.vector.tensor_copy, w_bf[u], w_raw[e, 1], u, W3_ON_SCALAR[e], P)
-            return w_bf
+        def words_over(e):
+            return reused.tile([P, C], U32, name=f"h_words{e}", align_bytes=64, offset=RAW_BYTES * e + WORDS_AT)
 
         x_word_window = x_words[:].bitcast(U32)
         slot_words = gather(x_word_window, U32, 0, 2, "words01")
@@ -189,49 +196,53 @@ def tile_moe_cap2_glu_gelu_kernel(tc, xT, w1, w3, w2, gate, offs, pos1, pos2, ou
         for e in range(E):
             w_bf = round_w1(e)
             if e > 0:
-                h_bf = hidden_tiles(e - 1)
+                h_bf = hidden_tile(e - 1)
                 for i in range(2):
                     multiply(h_bf, i, gelus, sums3)
-            sums1 = project(quantize_weights(w_bf, "w1"), e, "sums1")
+            banks = [f"bank{3 * (e % 2) + i}" for i in range(3)]
+            sums1 = project(quantize_weights(w_bf, "w1"), e, (banks[0], banks[1]))
             w_bf = round_w3(e)
-            gelus = gelu(sums1, w_raw[e, 1])
-            sums3 = project(quantize_weights(w_bf, "w3"), e, "sums3")
+            room = reused.tile([P, PACK, C], F32, name=f"gelu{e}", offset=RAW_BYTES * e + GELU_AT)
+            gelus = gelu(sums1, room)
+            sums3 = project(quantize_weights(w_bf, "w3"), e, (banks[2], banks[0]))
             if e == 0:
-                slot_words = slot_words + gather(x_word_window, U32, 2, 2, "w3_bf0")
-            else:
-                hidden.append(quantize_hidden(h_bf, f"w3_bf{e}"))
-            if 0 < e < last:
-                slot_scales = slot_scales + gather(x_scales[:], U8, e + 1, 1, f"h_bf{e - 1}0")
+                slot_words = slot_words + gather(x_word_window, U32, 2, 2, "words23", OTHER_AT)
+            elif e < last:
+                hidden.append(quantize_hidden(h_bf, [slice(0, C)], words_over(e)))
+                slot_scales = slot_scales + gather(x_scales[:], U8, e + 1, 1, f"scales{e + 1}", RAW_BYTES * e + OTHER_AT)
 
-        w2_bf = []
-        for pair, (copy, tag) in enumerate(((nc.vector.tensor_copy, f"before_w1_{E}"), (nc.scalar.copy, "w2_bf"))):
-            both = keep.tile([P, 2, N, PACK], BF16, name="w2_bf", tag=tag, align_bytes=64)
-            for i in range(2):
-                interleave(copy, both[:, i], w2_raw[pair][:, i])
-                w2_bf.append(both[:, i])
+        w2_bf = {}
+        for e in W2_ORDER:
+            on_vector = e == W2_ON_VECTOR
+            pool, offset = (reused, RAW_BYTES * last + OTHER_AT) if on_vector else (keep, None)
+            w2_bf[e] = pool.tile([P, N, PACK], BF16, name=f"w2_bf{e}", align_bytes=64, offset=offset)
+            interleave(nc.vector.tensor_copy if on_vector else nc.scalar.copy, w2_bf[e][:], w2_raw[e][:])
+            if on_vector:
+                hidden.append(quantize_hidden(h_bf, [slice(0, C)], words_over(last)))
 
         def quantize_w2(e):
             words = each.tile([P, N], U32, name="w2_words", align_bytes=64)
             scales = each.tile([P, N], U8, name="w2_scales", align_bytes=64)
-            quantize(words[:], scales[:], w2_bf[e].rearrange("p n j -> p (n j)"))
+            quantize(words[:], scales[:], w2_bf[e][:].rearrange("p n j -> p (n j)"))
             return words[:], scales[:]
 
-        h_bf = hidden_tiles(last)
+        h_bf = hidden_tile(last)
         multiply(h_bf, 0, gelus, sums3)
-        w2_mx = [quantize_w2(e) for e in range(last)]
+        w2_mx = {e: quantize_w2(e) for e in W2_ORDER[:last]}
         multiply(h_bf, 1, gelus, sums3)
-        w2_mx.append(quantize_w2(last))
-        hidden.append(quantize_hidden(h_bf, "h_words_last"))
+        w2_mx[W2_ORDER[last]] = quantize_w2(W2_ORDER[last])
+        last_words = keep.tile([P, C], U32, name="last_words", align_bytes=64)
+        hidden.append(quantize_hidden(h_bf, HALVES, last_words))
 
-        def second_layer(e, piece, copy):
-            acc = psum.tile([P, C], F32, name="acc", tag="sums1")
+        def second_layer(e, piece, copy, bank):
+            acc = psum.tile([P, C], F32, name="acc", tag=f"bank{bank}")
             product(acc[:, piece], w2_mx[e], (hidden[e][0][:, piece], hidden[e][1][:, piece]))
             copy(out=results[:, e * C + piece.start : e * C + piece.stop], in_=acc[:, piece])
 
         for e in range(last):
-            second_layer(e, slice(0, C), nc.scalar.copy)
-        second_layer(last, HALVES[0], nc.scalar.copy)
-        second_layer(last, HALVES[1], nc.vector.tensor_copy)
+            second_layer(e, slice(0, C), nc.scalar.copy, e)
+        second_layer(last, HALVES[0], nc.scalar.copy, 6)
+        second_layer(last, HALVES[1], nc.vector.tensor_copy, 7)
 
         first = keep.tile([P, T], F32, name="first")
         nc.vector.tensor_tensor(first[:], results[:].indirect(pos1_t[:]), gates[0][:], MULT)

@@ -115,16 +115,18 @@ def tile_moe_cap2_glu_gelu_kernel(tc, xT, w1, w3, w2, gate, offs, pos1, pos2, ou
             return [keep.tile([P, 2, P, PACK], BF16, name="w_bf", tag=tag, align_bytes=64) for tag in tags]
 
         def round_pair(copy, pairs, raw, u, lo, hi):
-            src = raw[:, :, PACK * lo : PACK * hi].rearrange("p (a b) (m u v) -> p u m a v b", b=2, u=PAIRS, v=2)
-            copy(out=pairs[u][:, :, lo:hi, :].rearrange("p v m (a b) -> p m a v b", b=2), in_=src[:, u])
+            src = raw[:, :, PACK * lo : PACK * hi].rearrange("p j (m u v) -> p u m j v", u=PAIRS, v=2)
+            copy(out=pairs[u][:, :, lo:hi, :].rearrange("p v m j -> p m j v"), in_=src[:, u])
+
+        def copy_on_gpsimd(out, in_):
+            nc.gpsimd.tensor_scalar(out, in_, 1.0, 0.0, MULT, ADD)
 
         def round_w1(e):
             raw, split = w_raw[e, 0], W1_ON_SCALAR
             pairs = pair_tiles([f"w1_bf{e}0", f"w1_bf{e}"])
             round_pair(nc.scalar.copy, pairs, raw, 0, 0, P)
             round_pair(nc.scalar.copy, pairs, raw, 1, 0, split)
-            src = raw[:, :, PACK * split : H].rearrange("p j (m u v) -> p u m v j", u=PAIRS, v=2)
-            nc.gpsimd.tensor_scalar(pairs[1][:, :, split:P, :].rearrange("p v m j -> p m v j"), src[:, 1], 1.0, 0.0, MULT, ADD)
+            round_pair(copy_on_gpsimd, pairs, raw, 1, split, P)
             return pairs
 
         def round_w3(e):

@@ -25,13 +25,14 @@ HALVES = (slice(0, P), slice(P, C))
 
 X_PIECES = (slice(0, 256), slice(256, 512), slice(512, T))
 
+PAIRS = 2
 W1_ON_SCALAR = 24
-W3_ON_SCALAR = (64, 64, 64, 56)
+W3_ON_SCALAR = 64
+LAST_W3_ON_SCALAR = 56
+W2_ON_VECTOR = 1
+
 RAW_BYTES = PACK * H * 4
 GELU_AT, WORDS_AT, OTHER_AT = 0, 4096, 5120
-PAIRS = 2
-W2_ORDER = (0, 1, 2, 3)
-W2_ON_VECTOR = 1
 
 
 def tile_moe_cap2_glu_gelu_kernel(tc, xT, w1, w3, w2, gate, offs, pos1, pos2, out):
@@ -57,9 +58,9 @@ def tile_moe_cap2_glu_gelu_kernel(tc, xT, w1, w3, w2, gate, offs, pos1, pos2, ou
                 else:
                     w_raw[e, which] = reused.tile([P, PACK, H], F32, name=f"w3_raw{e}", offset=RAW_BYTES * e)
                 nc.sync.dma_start(w_raw[e, which][:], w[e].rearrange("(p j) i -> p j i", j=PACK))
-        w2_raw = {}
-        for e in W2_ORDER:
-            w2_raw[e] = keep.tile([P, PACK, N], F32, name=f"w2_raw{e}")
+        w2_raw = []
+        for e in range(E):
+            w2_raw.append(keep.tile([P, PACK, N], F32, name=f"w2_raw{e}"))
             nc.sync.dma_start(w2_raw[e][:], w2[e].rearrange("(p j) n -> p j n", j=PACK))
         nc.sync.dma_start(pos1_t[:], pos1)
         nc.sync.dma_start(pos2_t[:], pos2)
@@ -122,32 +123,31 @@ def tile_moe_cap2_glu_gelu_kernel(tc, xT, w1, w3, w2, gate, offs, pos1, pos2, ou
             nc.gpsimd.tensor_scalar(out, in_, 1.0, 0.0, MULT, ADD)
 
         def round_w1(e):
-            raw, split = w_raw[e, 0], W1_ON_SCALAR
             pairs = pair_tiles([f"w1_bf{e}0", f"w1_bf{e}"])
-            round_pair(nc.scalar.copy, pairs, raw, 0, 0, P)
-            round_pair(nc.scalar.copy, pairs, raw, 1, 0, split)
-            round_pair(copy_on_gpsimd, pairs, raw, 1, split, P)
+            round_pair(nc.scalar.copy, pairs, w_raw[e, 0], 0, 0, P)
+            round_pair(nc.scalar.copy, pairs, w_raw[e, 0], 1, 0, W1_ON_SCALAR)
+            round_pair(copy_on_gpsimd, pairs, w_raw[e, 0], 1, W1_ON_SCALAR, P)
             return pairs
 
         def round_w3(e):
             pairs = pair_tiles([f"w3_bf{e}0", "w1_bf1" if e == 0 else f"w3_bf{e}1"])
-            for copy, lo, hi in ((nc.scalar.copy, 0, W3_ON_SCALAR[e]), (nc.vector.tensor_copy, W3_ON_SCALAR[e], P)):
+            split = LAST_W3_ON_SCALAR if e == E - 1 else W3_ON_SCALAR
+            for copy, lo, hi in ((nc.scalar.copy, 0, split), (nc.vector.tensor_copy, split, P)):
                 for u in range(PAIRS):
                     round_pair(copy, pairs, w_raw[e, 1], u, lo, hi)
             return pairs
 
-        def quantize_weights(parts, tag):
+        def quantize_weights(pairs, tag):
             weights = []
-            for u, w_bf in enumerate(parts):
-                tiles = w_bf.shape[1]
-                words = each.tile([P, tiles, P], U32, name="w_words", tag=f"{tag}_words{u}", align_bytes=64)
-                scales = each.tile([P, tiles, P], U8, name="w_scales", tag=f"{tag}_scales{u}", align_bytes=64)
+            for u, w_bf in enumerate(pairs):
+                words = each.tile([P, 2, P], U32, name="w_words", tag=f"{tag}_words{u}", align_bytes=64)
+                scales = each.tile([P, 2, P], U8, name="w_scales", tag=f"{tag}_scales{u}", align_bytes=64)
                 quantize(
-                    words[:].rearrange("p t m -> p (t m)"),
-                    scales[:].rearrange("p t m -> p (t m)"),
-                    w_bf[:].rearrange("p t m j -> p (t m j)"),
+                    words[:].rearrange("p v m -> p (v m)"),
+                    scales[:].rearrange("p v m -> p (v m)"),
+                    w_bf[:].rearrange("p v m j -> p (v m j)"),
                 )
-                weights.extend((words[:, t, :], scales[:, t, :]) for t in range(tiles))
+                weights.extend((words[:, v, :], scales[:, v, :]) for v in range(2))
             return weights
 
         def project(weights, e, tags):
@@ -214,13 +214,17 @@ def tile_moe_cap2_glu_gelu_kernel(tc, xT, w1, w3, w2, gate, offs, pos1, pos2, ou
                 slot_scales = slot_scales + gather(x_scales[:], U8, e + 1, 1, f"scales{e + 1}", RAW_BYTES * e + OTHER_AT)
 
         w2_bf = {}
-        for e in W2_ORDER:
-            on_vector = e == W2_ON_VECTOR
-            pool, offset = (reused, RAW_BYTES * last + OTHER_AT) if on_vector else (keep, None)
-            w2_bf[e] = pool.tile([P, N, PACK], BF16, name=f"w2_bf{e}", align_bytes=64, offset=offset)
-            interleave(nc.vector.tensor_copy if on_vector else nc.scalar.copy, w2_bf[e][:], w2_raw[e][:])
-            if on_vector:
+        for e in range(E):
+            if e == W2_ON_VECTOR:
+                w2_bf[e] = reused.tile([P, N, PACK], BF16, name="w2_bf", align_bytes=64, offset=RAW_BYTES * last + OTHER_AT)
+                interleave(nc.vector.tensor_copy, w2_bf[e][:], w2_raw[e][:])
                 hidden.append(quantize_hidden(h_bf, [slice(0, C)], words_over(last)))
+            elif e == last:
+                w2_bf[e] = keep.tile([P, N, PACK], BF16, name="w2_bf", tag=f"w1_bf{E}", align_bytes=64)
+                interleave(copy_on_gpsimd, w2_bf[e][:], w2_raw[e][:])
+            else:
+                w2_bf[e] = keep.tile([P, N, PACK], BF16, name=f"w2_bf{e}", align_bytes=64)
+                interleave(nc.scalar.copy, w2_bf[e][:], w2_raw[e][:])
 
         def quantize_w2(e):
             words = each.tile([P, N], U32, name="w2_words", align_bytes=64)
@@ -230,9 +234,9 @@ def tile_moe_cap2_glu_gelu_kernel(tc, xT, w1, w3, w2, gate, offs, pos1, pos2, ou
 
         h_bf = hidden_tile(last)
         multiply(h_bf, 0, gelus, sums3)
-        w2_mx = {e: quantize_w2(e) for e in W2_ORDER[:last]}
+        w2_mx = [quantize_w2(e) for e in range(last)]
         multiply(h_bf, 1, gelus, sums3)
-        w2_mx[W2_ORDER[last]] = quantize_w2(W2_ORDER[last])
+        w2_mx.append(quantize_w2(last))
         last_words = keep.tile([P, C], U32, name="last_words", align_bytes=64)
         hidden.append(quantize_hidden(h_bf, HALVES, last_words))
 

@@ -26,10 +26,9 @@ HALVES = (slice(0, P), slice(P, C))
 X_PIECES = (slice(0, 256), slice(256, 512), slice(512, T))
 
 PAIRS = 2
-W1_ON_SCALAR = 24
+W1_ON_SCALAR = 16
 W3_ON_SCALAR = 64
 LAST_W3_ON_SCALAR = 56
-W2_ON_VECTOR = 1
 
 RAW_BYTES = PACK * H * 4
 GELU_AT, WORDS_AT, OTHER_AT = 0, 4096, 5120
@@ -123,10 +122,10 @@ def tile_moe_cap2_glu_gelu_kernel(tc, xT, w1, w3, w2, gate, offs, pos1, pos2, ou
             nc.gpsimd.tensor_scalar(out, in_, 1.0, 0.0, MULT, ADD)
 
         def round_w1(e):
-            pairs = pair_tiles([f"w1_bf{e}0", f"w1_bf{e}"])
-            round_pair(nc.scalar.copy, pairs, w_raw[e, 0], 0, 0, P)
-            round_pair(nc.scalar.copy, pairs, w_raw[e, 0], 1, 0, W1_ON_SCALAR)
-            round_pair(copy_on_gpsimd, pairs, w_raw[e, 0], 1, W1_ON_SCALAR, P)
+            pairs = pair_tiles([f"w1_bf{e}", f"w1_bf{e}1"])
+            round_pair(nc.scalar.copy, pairs, w_raw[e, 0], 0, 0, W1_ON_SCALAR)
+            round_pair(nc.scalar.copy, pairs, w_raw[e, 0], 1, 0, P)
+            round_pair(copy_on_gpsimd, pairs, w_raw[e, 0], 0, W1_ON_SCALAR, P)
             return pairs
 
         def round_w3(e):
@@ -205,38 +204,37 @@ def tile_moe_cap2_glu_gelu_kernel(tc, xT, w1, w3, w2, gate, offs, pos1, pos2, ou
             sums1 = project(quantize_weights(w_bf, "w1"), e, (banks[0], banks[1]))
             w_bf = round_w3(e)
             room = reused.tile([P, PACK, C], F32, name=f"gelu{e}", offset=RAW_BYTES * e + GELU_AT)
+            if e == last:
+                early = keep.tile([P, 2, N, PACK], BF16, name="w2_early", align_bytes=64)
+                interleave(nc.scalar.copy, early[:, 0], w2_raw[0][:])
             gelus = gelu(sums1, room)
-            sums3 = project(quantize_weights(w_bf, "w3"), e, (banks[2], banks[0]))
+            sums3 = project(quantize_weights(w_bf, "w3"), e, (banks[2], banks[0] if e < last else "bank6"))
             if e == 0:
                 slot_words = slot_words + gather(x_word_window, U32, 2, 2, "words23", OTHER_AT)
             elif e < last:
                 hidden.append(quantize_hidden(h_bf, [slice(0, C)], words_over(e)))
                 slot_scales = slot_scales + gather(x_scales[:], U8, e + 1, 1, f"scales{e + 1}", RAW_BYTES * e + OTHER_AT)
 
-        w2_bf = {}
-        for e in range(E):
-            if e == W2_ON_VECTOR:
-                w2_bf[e] = reused.tile([P, N, PACK], BF16, name="w2_bf", align_bytes=64, offset=RAW_BYTES * last + OTHER_AT)
-                interleave(nc.vector.tensor_copy, w2_bf[e][:], w2_raw[e][:])
-                hidden.append(quantize_hidden(h_bf, [slice(0, C)], words_over(last)))
-            elif e == last:
-                w2_bf[e] = keep.tile([P, N, PACK], BF16, name="w2_bf", tag=f"w1_bf{E}", align_bytes=64)
-                interleave(copy_on_gpsimd, w2_bf[e][:], w2_raw[e][:])
-            else:
-                w2_bf[e] = keep.tile([P, N, PACK], BF16, name=f"w2_bf{e}", align_bytes=64)
-                interleave(nc.scalar.copy, w2_bf[e][:], w2_raw[e][:])
+        def quantize_w2(values, count, name):
+            words = keep.tile([P, count, N], U32, name=f"{name}_words", align_bytes=64)
+            scales = keep.tile([P, count, N], U8, name=f"{name}_scales", align_bytes=64)
+            quantize(
+                words[:].rearrange("p e n -> p (e n)"),
+                scales[:].rearrange("p e n -> p (e n)"),
+                values.rearrange("p e n j -> p (e n j)"),
+            )
+            return [(words[:, i, :], scales[:, i, :]) for i in range(count)]
 
-        def quantize_w2(e):
-            words = each.tile([P, N], U32, name="w2_words", align_bytes=64)
-            scales = each.tile([P, N], U8, name="w2_scales", align_bytes=64)
-            quantize(words[:], scales[:], w2_bf[e][:].rearrange("p n j -> p (n j)"))
-            return words[:], scales[:]
-
+        interleave(nc.vector.tensor_copy, early[:, 1], w2_raw[1][:])
+        hidden.append(quantize_hidden(h_bf, [slice(0, C)], words_over(last)))
+        w2_mx = quantize_w2(early[:], 2, "early")
+        late = keep.tile([P, 2, N, PACK], BF16, name="w2_bf", tag=f"w1_bf{E}", align_bytes=64)
+        interleave(nc.scalar.copy, late[:, 0], w2_raw[2][:])
+        interleave(copy_on_gpsimd, late[:, 1], w2_raw[last][:])
         h_bf = hidden_tile(last)
         multiply(h_bf, 0, gelus, sums3)
-        w2_mx = [quantize_w2(e) for e in range(last)]
         multiply(h_bf, 1, gelus, sums3)
-        w2_mx.append(quantize_w2(last))
+        w2_mx = w2_mx + quantize_w2(late[:], 2, "late")
         last_words = keep.tile([P, C], U32, name="last_words", align_bytes=64)
         hidden.append(quantize_hidden(h_bf, HALVES, last_words))
 
@@ -247,7 +245,7 @@ def tile_moe_cap2_glu_gelu_kernel(tc, xT, w1, w3, w2, gate, offs, pos1, pos2, ou
 
         for e in range(last):
             second_layer(e, slice(0, C), nc.scalar.copy, e)
-        second_layer(last, HALVES[0], nc.scalar.copy, 6)
+        second_layer(last, HALVES[0], nc.scalar.copy, 3)
         second_layer(last, HALVES[1], nc.vector.tensor_copy, 7)
 
         first = keep.tile([P, T], F32, name="first")

@@ -61,10 +61,9 @@ def tile_moe_cap2_glu_gelu_kernel(tc, xT, w1, w3, w2, gate, offs, pos1, pos2, ou
         for e in range(E):
             w2_raw.append(keep.tile([P, PACK, N], F32, name=f"w2_raw{e}"))
             nc.sync.dma_start(w2_raw[e][:], w2[e].rearrange("(p j) n -> p j n", j=PACK))
-        nc.sync.dma_start(pos1_t[:], pos1)
-        nc.sync.dma_start(pos2_t[:], pos2)
         gates = []
-        for choice in range(2):
+        for choice, (pos_t, pos) in enumerate(((pos1_t, pos1), (pos2_t, pos2))):
+            nc.sync.dma_start(pos_t[:], pos)
             gates.append(keep.tile([P, T], F32, name=f"gate{choice}"))
             nc.sync.dma_start(gates[choice][:], gate[choice])
 
@@ -229,8 +228,8 @@ def tile_moe_cap2_glu_gelu_kernel(tc, xT, w1, w3, w2, gate, offs, pos1, pos2, ou
         hidden.append(quantize_hidden(h_bf, [slice(0, C)], words_over(last)))
         w2_mx = quantize_w2(early[:], 2, "early")
         late = keep.tile([P, 2, N, PACK], BF16, name="w2_bf", tag=f"w1_bf{E}", align_bytes=64)
-        interleave(nc.scalar.copy, late[:, 0], w2_raw[2][:])
-        interleave(copy_on_gpsimd, late[:, 1], w2_raw[last][:])
+        interleave(copy_on_gpsimd, late[:, 0], w2_raw[2][:])
+        interleave(nc.scalar.copy, late[:, 1], w2_raw[last][:])
         h_bf = hidden_tile(last)
         multiply(h_bf, 0, gelus, sums3)
         multiply(h_bf, 1, gelus, sums3)

@@ -30,6 +30,7 @@ W1_ON_SCALAR = 16
 W3_ON_SCALAR = 64
 LAST_W3_ON_SCALAR = 56
 
+ROW_ALIGN = 512
 RAW_BYTES = PACK * H * 4
 GELU_AT, WORDS_AT, OTHER_AT = 0, 4096, 5120
 
@@ -46,25 +47,27 @@ def tile_moe_cap2_glu_gelu_kernel(tc, xT, w1, w3, w2, gate, offs, pos1, pos2, ou
         offs_t = lists.tile([P, S // LIST], U16, name="offs_t")
         pos1_t = lists.tile([P, T // LIST], U16, name="pos1_t")
         pos2_t = lists.tile([P, T // LIST], U16, name="pos2_t")
-        x_raw = keep.tile([P, PACK, T], F32, name="x_raw")
+        x_raw = keep.tile([P, PACK, T], F32, name="x_raw", align_bytes=ROW_ALIGN)
         nc.sync.dma_start(x_raw[:], xT.rearrange("(p j) t -> p j t", j=PACK))
         nc.sync.dma_start(offs_t[:], offs)
         w_raw = {}
         for e in range(E):
             for which, w in enumerate((w1, w3)):
                 if which == 0:
-                    w_raw[e, which] = keep.tile([P, PACK, H], F32, name=f"w1_raw{e}")
+                    w_raw[e, which] = keep.tile([P, PACK, H], F32, name=f"w1_raw{e}", align_bytes=ROW_ALIGN)
                 else:
-                    w_raw[e, which] = reused.tile([P, PACK, H], F32, name=f"w3_raw{e}", offset=RAW_BYTES * e)
+                    w_raw[e, which] = reused.tile(
+                        [P, PACK, H], F32, name=f"w3_raw{e}", align_bytes=ROW_ALIGN, offset=RAW_BYTES * e
+                    )
                 nc.sync.dma_start(w_raw[e, which][:], w[e].rearrange("(p j) i -> p j i", j=PACK))
         w2_raw = []
         for e in range(E):
-            w2_raw.append(keep.tile([P, PACK, N], F32, name=f"w2_raw{e}"))
+            w2_raw.append(keep.tile([P, PACK, N], F32, name=f"w2_raw{e}", align_bytes=ROW_ALIGN))
             nc.sync.dma_start(w2_raw[e][:], w2[e].rearrange("(p j) n -> p j n", j=PACK))
         gates = []
         for choice, (pos_t, pos) in enumerate(((pos1_t, pos1), (pos2_t, pos2))):
             nc.sync.dma_start(pos_t[:], pos)
-            gates.append(keep.tile([P, T], F32, name=f"gate{choice}"))
+            gates.append(keep.tile([P, T], F32, name=f"gate{choice}", align_bytes=ROW_ALIGN))
             nc.sync.dma_start(gates[choice][:], gate[choice])
 
         x_scales = keep.tile([P, WINDOW], U8, name="x_scales", align_bytes=64)
@@ -256,6 +259,6 @@ def tile_moe_cap2_glu_gelu_kernel(tc, xT, w1, w3, w2, gate, offs, pos1, pos2, ou
             columns = slice(tokens.start // LIST, tokens.stop // LIST)
             nc.vector.tensor_tensor(second[i][:], results[:].indirect(pos2_t[:, columns]), gates[1][:, tokens], MULT)
         for i, tokens in enumerate(token_halves):
-            total = keep.tile([P, T // 2], F32, name=f"total{i}")
+            total = keep.tile([P, T // 2], F32, name=f"total{i}", align_bytes=ROW_ALIGN)
             nc.vector.tensor_tensor(total[:], first[:, tokens], second[i][:], ADD)
             nc.sync.dma_start(out[:, tokens], total[:])

@@ -11,6 +11,7 @@ U8 = mybir.dt.uint8
 FP8X4 = mybir.dt.float8_e4m3fn_x4
 MULT = mybir.AluOpType.mult
 ADD = mybir.AluOpType.add
+COPY = mybir.ActivationFunctionType.Copy
 GELU = mybir.ActivationFunctionType.Gelu_apprx_tanh
 
 P = 128
@@ -247,8 +248,8 @@ def tile_moe_cap2_glu_gelu_kernel(tc, xT, w1, w3, w2, gate, offs, pos1, pos2, ou
 
         for e in range(last):
             second_layer(e, slice(0, C), nc.scalar.copy, e)
-        second_layer(last, HALVES[0], nc.scalar.copy, 3)
-        second_layer(last, HALVES[1], nc.vector.tensor_copy, 7)
+        second_layer(last, HALVES[0], nc.vector.tensor_copy, 3)
+        second_layer(last, HALVES[1], nc.scalar.copy, 7)
 
         first = keep.tile([P, T], F32, name="first")
         nc.vector.tensor_tensor(first[:], results[:].indirect(pos1_t[:]), gates[0][:], MULT)

@@ -31,6 +31,8 @@ W1_ON_SCALAR = 16
 W3_ON_SCALAR = 64
 LAST_W3_ON_SCALAR = 56
 
+OUT_PIECES = (slice(0, 128), slice(128, 384), slice(384, 544), slice(544, T))
+
 ROW_ALIGN = 512
 RAW_BYTES = PACK * H * 4
 GELU_AT, WORDS_AT, OTHER_AT = 0, 4096, 5120
@@ -237,7 +239,8 @@ def tile_moe_cap2_glu_gelu_kernel(tc, xT, w1, w3, w2, gate, offs, pos1, pos2, ou
         h_bf = hidden_tile(last)
         multiply(h_bf, 0, gelus, sums3)
         multiply(h_bf, 1, gelus, sums3)
-        w2_mx = w2_mx + quantize_w2(late[:], 2, "late")
+        for i in range(2):
+            w2_mx = w2_mx + quantize_w2(late[:, i : i + 1], 1, f"late{i}")
         last_words = keep.tile([P, C], U32, name="last_words", align_bytes=64)
         hidden.append(quantize_hidden(h_bf, HALVES, last_words))
 
@@ -247,19 +250,41 @@ def tile_moe_cap2_glu_gelu_kernel(tc, xT, w1, w3, w2, gate, offs, pos1, pos2, ou
             copy(out=results[:, e * C + piece.start : e * C + piece.stop], in_=acc[:, piece])
 
         for e in range(last):
-            second_layer(e, slice(0, C), nc.scalar.copy, e)
-        second_layer(last, HALVES[0], nc.vector.tensor_copy, 3)
+            second_layer(e, slice(0, C), nc.scalar.copy if e < last - 1 else nc.vector.tensor_copy, e)
+        second_layer(last, HALVES[0], nc.scalar.copy, 3)
         second_layer(last, HALVES[1], nc.scalar.copy, 7)
 
-        first = keep.tile([P, T], F32, name="first")
-        nc.vector.tensor_tensor(first[:], results[:].indirect(pos1_t[:]), gates[0][:], MULT)
-        token_halves = (slice(0, T // 2), slice(T // 2, T))
-        second = []
-        for i, tokens in enumerate(token_halves):
-            second.append(keep.tile([P, T // 2], F32, name=f"second{i}"))
+        def fetch(pos_t, tokens, name):
+            picked = keep.tile([P, tokens.stop - tokens.start], F32, name=name)
             columns = slice(tokens.start // LIST, tokens.stop // LIST)
-            nc.vector.tensor_tensor(second[i][:], results[:].indirect(pos2_t[:, columns]), gates[1][:, tokens], MULT)
-        for i, tokens in enumerate(token_halves):
-            total = keep.tile([P, T // 2], F32, name=f"total{i}", align_bytes=ROW_ALIGN)
-            nc.vector.tensor_tensor(total[:], first[:, tokens], second[i][:], ADD)
+            nc.scalar.activation(picked[:], results[:].indirect(pos_t[:, columns]), COPY)
+            return picked
+
+        def weigh(picked, choice, tokens, name):
+            weighed = keep.tile([P, tokens.stop - tokens.start], F32, name=name)
+            nc.vector.tensor_tensor(weighed[:], picked, gates[choice][:, tokens], MULT)
+            return weighed
+
+        def add_and_store(first, second, tokens, name):
+            total = keep.tile([P, tokens.stop - tokens.start], F32, name=name, align_bytes=ROW_ALIGN)
+            nc.vector.tensor_tensor(total[:], first, second, ADD)
             nc.sync.dma_start(out[:, tokens], total[:])
+
+        a, b, c, d = OUT_PIECES
+        head = slice(0, c.start)
+        first_head = weigh(results[:].indirect(pos1_t[:, 0 : c.start // LIST]), 0, head, "first_head")
+        picked = {}
+        for name, tokens in zip("abcd", OUT_PIECES):
+            if tokens.start >= c.start:
+                picked[name, 0] = fetch(pos1_t, tokens, f"picked_first_{name}")
+            picked[name, 1] = fetch(pos2_t, tokens, f"picked_second_{name}")
+        second_a = weigh(picked["a", 1][:], 1, a, "second_a")
+        second_b = weigh(picked["b", 1][:], 1, b, "second_b")
+        add_and_store(first_head[:, a], second_a[:], a, "total_a")
+        first_c = weigh(picked["c", 0][:], 0, c, "first_c")
+        add_and_store(first_head[:, b], second_b[:], b, "total_b")
+        second_c = weigh(picked["c", 1][:], 1, c, "second_c")
+        first_d = weigh(picked["d", 0][:], 0, d, "first_d")
+        second_d = weigh(picked["d", 1][:], 1, d, "second_d")
+        add_and_store(first_c[:], second_c[:], c, "total_c")
+        add_and_store(first_d[:], second_d[:], d, "total_d")

from contextlib import ExitStack

import concourse.mybir as mybir

F32 = mybir.dt.float32
BF16 = mybir.dt.bfloat16
I32 = mybir.dt.int32
U32 = mybir.dt.uint32
U16 = mybir.dt.uint16
U8 = mybir.dt.uint8
FP8X4 = mybir.dt.float8_e4m3fn_x4
MULT = mybir.AluOpType.mult
ADD = mybir.AluOpType.add
COPY = mybir.ActivationFunctionType.Copy
GELU = mybir.ActivationFunctionType.Gelu_apprx_tanh

P = 128
PACK = 4
LIST = 16
K, T, E, C, H, N = 512, 640, 4, 256, 512, 128
S = E * C
PAD = 32
WINDOW = 704
FLOPS = 2 * S * K * H * 2 + 2 * S * H * N
HALVES = (slice(0, P), slice(P, C))

X_PIECES = (slice(0, 256), slice(256, 512), slice(512, T))

PAIRS = 2
W1_ON_SCALAR = 16
W3_ON_SCALAR = 64
LAST_W3_ON_SCALAR = 56

OUT_PIECES = (slice(0, 128), slice(128, 384), slice(384, 544), slice(544, T))

ROW_ALIGN = 512
RAW_BYTES = PACK * H * 4
GELU_AT, WORDS_AT, OTHER_AT = 0, 4096, 5120


def tile_moe_cap2_glu_gelu_kernel(tc, xT, w1, w3, w2, gate, offs, pos1, pos2, out):
    nc = tc.nc
    with ExitStack() as ctx:
        lists = ctx.enter_context(tc.tile_pool(name="lists", bufs=1))
        keep = ctx.enter_context(tc.tile_pool(name="keep", bufs=1))
        reused = ctx.enter_context(tc.tile_pool(name="reused", bufs=1))
        each = ctx.enter_context(tc.tile_pool(name="each", bufs=E))
        psum = ctx.enter_context(tc.psum_pool(name="psum", bufs=1))

        offs_t = lists.tile([P, S // LIST], U16, name="offs_t")
        pos1_t = lists.tile([P, T // LIST], U16, name="pos1_t")
        pos2_t = lists.tile([P, T // LIST], U16, name="pos2_t")
        x_raw = keep.tile([P, PACK, T], F32, name="x_raw", align_bytes=ROW_ALIGN)
        nc.sync.dma_start(x_raw[:], xT.rearrange("(p j) t -> p j t", j=PACK))
        nc.sync.dma_start(offs_t[:], offs)
        w_raw = {}
        for e in range(E):
            for which, w in enumerate((w1, w3)):
                if which == 0:
                    w_raw[e, which] = keep.tile([P, PACK, H], F32, name=f"w1_raw{e}", align_bytes=ROW_ALIGN)
                else:
                    w_raw[e, which] = reused.tile(
                        [P, PACK, H], F32, name=f"w3_raw{e}", align_bytes=ROW_ALIGN, offset=RAW_BYTES * e
                    )
                nc.sync.dma_start(w_raw[e, which][:], w[e].rearrange("(p j) i -> p j i", j=PACK))
        w2_raw = []
        for e in range(E):
            w2_raw.append(keep.tile([P, PACK, N], F32, name=f"w2_raw{e}", align_bytes=ROW_ALIGN))
            nc.sync.dma_start(w2_raw[e][:], w2[e].rearrange("(p j) n -> p j n", j=PACK))
        gates = []
        for choice, (pos_t, pos) in enumerate(((pos1_t, pos1), (pos2_t, pos2))):
            nc.sync.dma_start(pos_t[:], pos)
            gates.append(keep.tile([P, T], F32, name=f"gate{choice}", align_bytes=ROW_ALIGN))
            nc.sync.dma_start(gates[choice][:], gate[choice])

        x_scales = keep.tile([P, WINDOW], U8, name="x_scales", align_bytes=64)
        nc.gpsimd.memset(x_scales[:], 0)
        x_words = keep.tile([P, WINDOW], I32, name="x_words", align_bytes=64)
        nc.vector.memset(x_words[:, T:WINDOW], 0)
        results = keep.tile([P, S + PAD], F32, name="results")
        zeros = keep.tile([P, PAD], F32, name="zeros")
        nc.vector.memset(zeros[:], 0.0)
        nc.scalar.activation(out=results[:, S : S + PAD], in_=zeros[:], func=GELU)

        def quantize(words, scales, values):
            nc.vector.quantize_mx(out=words.bitcast(FP8X4), scales=scales, in_=values)

        def product(acc, weights, moving):
            nc.tensor.matmul_mx(
                out=acc,
                lhsT=weights[0].bitcast(FP8X4),
                lhsT_scale=weights[1],
                rhs=moving[0].bitcast(FP8X4),
                rhs_scale=moving[1],
                start=True,
                stop=True,
            )

        def interleave(copy, dst, src):
            copy(
                out=dst.rearrange("p (c i) j -> p c j i", i=PACK),
                in_=src.rearrange("p j (c i) -> p c j i", i=PACK),
            )

        x_bf = keep.tile([P, T, PACK], BF16, name="x_bf", tag="w1_bf0", align_bytes=64)
        interleave(nc.scalar.copy, x_bf[:, X_PIECES[0], :], x_raw[:, :, X_PIECES[0]])
        for piece in X_PIECES[1:]:
            interleave(nc.vector.tensor_copy, x_bf[:, piece, :], x_raw[:, :, piece])
        for piece in X_PIECES[1:] + X_PIECES[:1]:
            quantize(x_words[:, piece], x_scales[:, piece], x_bf[:, piece, :].rearrange("p t j -> p (t j)"))

        def gather(window, dtype, first, count, name, offset=None):
            pool = keep if offset is None else reused
            picked = pool.tile([P, count * C], dtype, name=name, align_bytes=64, offset=offset)
            columns = slice(first * C // LIST, (first + count) * C // LIST)
            nc.vector.tensor_copy(picked[:], window.indirect(offs_t[:, columns]))
            return [picked[:, i * C : (i + 1) * C] for i in range(count)]

        def pair_tiles(tags):
            return [keep.tile([P, 2, P, PACK], BF16, name="w_bf", tag=tag, align_bytes=64) for tag in tags]

        def round_pair(copy, pairs, raw, u, lo, hi):
            src = raw[:, :, PACK * lo : PACK * hi].rearrange("p j (m u v) -> p u m j v", u=PAIRS, v=2)
            copy(out=pairs[u][:, :, lo:hi, :].rearrange("p v m j -> p m j v"), in_=src[:, u])

        def copy_on_gpsimd(out, in_):
            nc.gpsimd.tensor_scalar(out, in_, 1.0, 0.0, MULT, ADD)

        def round_w1(e):
            pairs = pair_tiles([f"w1_bf{e}", f"w1_bf{e}1"])
            round_pair(nc.scalar.copy, pairs, w_raw[e, 0], 0, 0, W1_ON_SCALAR)
            round_pair(nc.scalar.copy, pairs, w_raw[e, 0], 1, 0, P)
            round_pair(copy_on_gpsimd, pairs, w_raw[e, 0], 0, W1_ON_SCALAR, P)
            return pairs

        def round_w3(e):
            pairs = pair_tiles([f"w3_bf{e}0", "w1_bf1" if e == 0 else f"w3_bf{e}1"])
            split = LAST_W3_ON_SCALAR if e == E - 1 else W3_ON_SCALAR
            for copy, lo, hi in ((nc.scalar.copy, 0, split), (nc.vector.tensor_copy, split, P)):
                for u in range(PAIRS):
                    round_pair(copy, pairs, w_raw[e, 1], u, lo, hi)
            return pairs

        def quantize_weights(pairs, tag):
            weights = []
            for u, w_bf in enumerate(pairs):
                words = each.tile([P, 2, P], U32, name="w_words", tag=f"{tag}_words{u}", align_bytes=64)
                scales = each.tile([P, 2, P], U8, name="w_scales", tag=f"{tag}_scales{u}", align_bytes=64)
                quantize(
                    words[:].rearrange("p v m -> p (v m)"),
                    scales[:].rearrange("p v m -> p (v m)"),
                    w_bf[:].rearrange("p v m j -> p (v m j)"),
                )
                weights.extend((words[:, v, :], scales[:, v, :]) for v in range(2))
            return weights

        def project(weights, e, tags):
            banks = []
            for half, tag in zip(HALVES, tags):
                acc = psum.tile([P, PACK, P], F32, name="acc", tag=tag)
                for t in range(PACK) if half.start == 0 else (2, 3, 0, 1):
                    product(acc[:, t, :], weights[t], (slot_words[e][:, half], slot_scales[e][:, half]))
                banks.append(acc)
            return banks

        def by_slot(bank):
            return bank[:].rearrange("p t (r n) -> p r n t", r=PACK)

        def gelu(banks, room):
            gelus = []
            for i, bank in enumerate(banks):
                gelus.append(room[:, :, i * P : (i + 1) * P].rearrange("p r (n t) -> p r n t", t=PACK))
                nc.scalar.activation(out=gelus[i], in_=by_slot(bank), func=GELU)
            return gelus

        def multiply(h_bf, i, gelus, banks):
            nc.vector.tensor_tensor(
                out=h_bf[:, HALVES[i], :].rearrange("p (r n) t -> p r n t", r=PACK),
                in0=gelus[i],
                in1=by_slot(banks[i]),
                op=MULT,
            )

        def hidden_tile(e):
            return keep.tile([P, C, PACK], BF16, name="h_bf", tag=f"w1_bf{e + 2}", align_bytes=64)

        def quantize_hidden(h_bf, pieces, words):
            scales = each.tile([P, C], U8, name="h_scales", align_bytes=64)
            for piece in pieces:
                quantize(words[:, piece], scales[:, piece], h_bf[:, piece, :].rearrange("p n t -> p (n t)"))
            return words, scales

        def words_over(e):
            return reused.tile([P, C], U32, name=f"h_words{e}", align_bytes=64, offset=RAW_BYTES * e + WORDS_AT)

        x_word_window = x_words[:].bitcast(U32)
        slot_words = gather(x_word_window, U32, 0, 2, "words01")
        slot_scales = gather(x_scales[:], U8, 0, 2, "scales01")
        last = E - 1
        hidden = []
        sums3 = gelus = None
        for e in range(E):
            w_bf = round_w1(e)
            if e > 0:
                h_bf = hidden_tile(e - 1)
                for i in range(2):
                    multiply(h_bf, i, gelus, sums3)
            banks = [f"bank{3 * (e % 2) + i}" for i in range(3)]
            sums1 = project(quantize_weights(w_bf, "w1"), e, (banks[0], banks[1]))
            w_bf = round_w3(e)
            room = reused.tile([P, PACK, C], F32, name=f"gelu{e}", offset=RAW_BYTES * e + GELU_AT)
            if e == last:
                early = keep.tile([P, 2, N, PACK], BF16, name="w2_early", align_bytes=64)
                interleave(nc.scalar.copy, early[:, 0], w2_raw[0][:])
            gelus = gelu(sums1, room)
            sums3 = project(quantize_weights(w_bf, "w3"), e, (banks[2], banks[0] if e < last else "bank6"))
            if e == 0:
                slot_words = slot_words + gather(x_word_window, U32, 2, 2, "words23", OTHER_AT)
            elif e < last:
                hidden.append(quantize_hidden(h_bf, [slice(0, C)], words_over(e)))
                slot_scales = slot_scales + gather(x_scales[:], U8, e + 1, 1, f"scales{e + 1}", RAW_BYTES * e + OTHER_AT)

        def quantize_w2(values, count, name):
            words = keep.tile([P, count, N], U32, name=f"{name}_words", align_bytes=64)
            scales = keep.tile([P, count, N], U8, name=f"{name}_scales", align_bytes=64)
            quantize(
                words[:].rearrange("p e n -> p (e n)"),
                scales[:].rearrange("p e n -> p (e n)"),
                values.rearrange("p e n j -> p (e n j)"),
            )
            return [(words[:, i, :], scales[:, i, :]) for i in range(count)]

        interleave(nc.vector.tensor_copy, early[:, 1], w2_raw[1][:])
        hidden.append(quantize_hidden(h_bf, [slice(0, C)], words_over(last)))
        w2_mx = quantize_w2(early[:], 2, "early")
        late = keep.tile([P, 2, N, PACK], BF16, name="w2_bf", tag=f"w1_bf{E}", align_bytes=64)
        interleave(copy_on_gpsimd, late[:, 0], w2_raw[2][:])
        interleave(nc.scalar.copy, late[:, 1], w2_raw[last][:])
        h_bf = hidden_tile(last)
        multiply(h_bf, 0, gelus, sums3)
        multiply(h_bf, 1, gelus, sums3)
        for i in range(2):
            w2_mx = w2_mx + quantize_w2(late[:, i : i + 1], 1, f"late{i}")
        last_words = keep.tile([P, C], U32, name="last_words", align_bytes=64)
        hidden.append(quantize_hidden(h_bf, HALVES, last_words))

        def second_layer(e, piece, copy, bank):
            acc = psum.tile([P, C], F32, name="acc", tag=f"bank{bank}")
            product(acc[:, piece], w2_mx[e], (hidden[e][0][:, piece], hidden[e][1][:, piece]))
            copy(out=results[:, e * C + piece.start : e * C + piece.stop], in_=acc[:, piece])

        for e in range(last):
            second_layer(e, slice(0, C), nc.scalar.copy if e < last - 1 else nc.vector.tensor_copy, e)
        second_layer(last, HALVES[0], nc.scalar.copy, 3)
        second_layer(last, HALVES[1], nc.scalar.copy, 7)

        def fetch(pos_t, tokens, name):
            picked = keep.tile([P, tokens.stop - tokens.start], F32, name=name)
            columns = slice(tokens.start // LIST, tokens.stop // LIST)
            nc.scalar.activation(picked[:], results[:].indirect(pos_t[:, columns]), COPY)
            return picked

        def weigh(picked, choice, tokens, name):
            weighed = keep.tile([P, tokens.stop - tokens.start], F32, name=name)
            nc.vector.tensor_tensor(weighed[:], picked, gates[choice][:, tokens], MULT)
            return weighed

        def add_and_store(first, second, tokens, name):
            total = keep.tile([P, tokens.stop - tokens.start], F32, name=name, align_bytes=ROW_ALIGN)
            nc.vector.tensor_tensor(total[:], first, second, ADD)
            nc.sync.dma_start(out[:, tokens], total[:])

        a, b, c, d = OUT_PIECES
        head = slice(0, c.start)
        first_head = weigh(results[:].indirect(pos1_t[:, 0 : c.start // LIST]), 0, head, "first_head")
        picked = {}
        for name, tokens in zip("abcd", OUT_PIECES):
            if tokens.start >= c.start:
                picked[name, 0] = fetch(pos1_t, tokens, f"picked_first_{name}")
            picked[name, 1] = fetch(pos2_t, tokens, f"picked_second_{name}")
        second_a = weigh(picked["a", 1][:], 1, a, "second_a")
        second_b = weigh(picked["b", 1][:], 1, b, "second_b")
        add_and_store(first_head[:, a], second_a[:], a, "total_a")
        first_c = weigh(picked["c", 0][:], 0, c, "first_c")
        add_and_store(first_head[:, b], second_b[:], b, "total_b")
        second_c = weigh(picked["c", 1][:], 1, c, "second_c")
        first_d = weigh(picked["d", 0][:], 0, d, "first_d")
        second_d = weigh(picked["d", 1][:], 1, d, "second_d")
        add_and_store(first_c[:], second_c[:], c, "total_c")
        add_and_store(first_d[:], second_d[:], d, "total_d")
